import numpy as np
import ml_dtypes


def mxq(x, axis, fmt="e4m3"):
    dtype, down = {"e4m3": (ml_dtypes.float8_e4m3fn, 7), "e5m2": (ml_dtypes.float8_e5m2, 14)}[fmt]
    v = np.moveaxis(np.asarray(x, np.float32).astype(ml_dtypes.bfloat16).astype(np.float64), axis, -1)
    blocks = v.reshape(v.shape[:-1] + (-1, 32))
    amax = np.abs(blocks).max(-1, keepdims=True)
    byte = np.maximum(np.where(amax > 0, np.frexp(amax)[1] - 1 + 127, 0) - down, 1)
    scale = np.exp2(byte - 127.0)
    codes = (blocks / scale).astype(np.float32).astype(dtype).astype(np.float64)
    return np.moveaxis((codes * scale).reshape(v.shape), -1, axis)


WIDE = False


def mx_kscale(k):
    if not WIDE:
        return np.ones(k)
    levels = np.array([10, -10, 5, -5, 0])
    if k % 512:
        return np.exp2(np.random.permutation(np.resize(levels, k // 32))).repeat(32)
    a = np.empty((k // 512, 16))
    for p in range(k // 512):
        a[p, :8] = np.random.permutation(np.resize(levels, 8))
        for g in range(8):
            far = levels[np.abs(levels - a[p, g]) >= 10]
            a[p, g + 8] = far[np.random.randint(len(far))]
    return np.exp2(a.ravel()).repeat(32)


def f64(x):
    return np.asarray(x).astype(np.float64)


def striped(idx):
    return np.tile(idx.reshape(-1, 16).T, (8, 1)).astype(np.uint16)


def unstriped(offs):
    return offs[:16].T.reshape(-1).astype(np.int64)


E2M1 = np.array([0.0, 0.5, 1.0, 1.5, 2.0, 3.0, 4.0, 6.0, -0.0, -0.5, -1.0, -1.5, -2.0, -3.0, -4.0, -6.0])


def pack_fp4(w):
    k, n = w.shape
    w = f64(np.asarray(w, np.float32).astype(ml_dtypes.bfloat16)).reshape(k // 32, 32, n)
    amax = np.abs(w).max(1)
    mant, ex = np.frexp(amax / 6.0)
    byte = np.clip(np.where(amax > 0, np.where(mant > 0.5, ex, ex - 1) + 127, 1), 1, 254)
    scaled = (w * np.exp2(127.0 - byte)[:, None, :]).reshape(k, n).astype(np.float32)
    c = np.ascontiguousarray(scaled.reshape(k // 512, 128, 4, n).transpose(0, 1, 3, 2)).astype(ml_dtypes.float4_e2m1fn).view(np.uint8) & 0xF
    words = (c[..., 0::2] | (c[..., 1::2] << 4)).reshape(k // 512, 128, 2 * n)
    return np.ascontiguousarray(words), np.ascontiguousarray(byte.astype(np.uint8).reshape(k // 512, 16, n))


def unpack_fp4(words, scales):
    g, _, n = scales.shape
    words = np.ascontiguousarray(words).reshape(g, 128, n, 2)
    nib = np.empty((g, 128, n, 4), np.uint8)
    nib[..., 0::2] = words & 0xF
    nib[..., 1::2] = words >> 4
    vals = E2M1[nib] * np.repeat(np.exp2(scales.astype(np.float64) - 127.0), 8, axis=1)[..., None]
    return vals.transpose(0, 1, 3, 2).reshape(g * 512, n)


def relu(v):
    return np.maximum(v, 0.0)


K, T, S, V, H, N = 512, 4096, 1024, 512, 512, 256


def setup_inputs():
    n = np.random.standard_normal
    s = mx_kscale(K)[:, None]
    u = mx_kscale(H)
    packed_w2 = pack_fp4(n((H, N)) / np.sqrt(H) / u[:, None])
    return {
        "xT": (n((K, T)) * s).astype(np.float32),
        "w1": (n((K, H)) / np.sqrt(K) / s * u).astype(np.float32),
        "w2_words": packed_w2[0],
        "w2_scales": packed_w2[1],
        "offs": striped(np.random.permutation(T)[:S]),
    }


def reference(xT, w1, w2_words, w2_scales, offs):
    xq = mxq(f64(xT)[:, unstriped(offs)], 0, "e4m3")
    h = relu(mxq(f64(w1), 0, "e4m3").T @ xq)
    z = np.abs(h[:, :V] - h[:, V:2 * V])
    return unpack_fp4(w2_words, w2_scales).T @ mxq(z, 0, "e4m3")

@@ -1,0 +1,134 @@
+from contextlib import ExitStack
+
+import concourse.mybir as mybir
+
+K, T, S, V, H, N = 512, 4096, 1024, 512, 512, 256
+FLOPS = 2 * K * H * S + 2 * H * N * V
+
+F32 = mybir.dt.float32
+BF16 = mybir.dt.bfloat16
+I32 = mybir.dt.int32
+U32 = mybir.dt.uint32
+U16 = mybir.dt.uint16
+U8 = mybir.dt.uint8
+FP8X4 = mybir.dt.float8_e4m3fn_x4
+FP4X4 = mybir.dt.float4_e2m1fn_x4
+ACT = mybir.ActivationFunctionType
+ALU = mybir.AluOpType
+
+P = 128
+PACK = 4
+CH = 128
+NCH = V // CH
+ABS_ON_SCALAR = [0]
+LAST_CHUNKS = [[4096,"v"]]
+W_PARTS = [[64,"s"],[64,"s"]]
+
+
+def tile_picked_siam_abs_e_kernel(tc, xT, w1, w2_words, w2_scales, offs, out):
+    nc = tc.nc
+    with ExitStack() as ctx:
+        keep = ctx.enter_context(tc.tile_pool(name="keep", bufs=1))
+        ring = ctx.enter_context(tc.tile_pool(name="ring", bufs=NCH))
+        psum = ctx.enter_context(tc.psum_pool(name="psum", bufs=8))
+
+        offsets = keep.tile([P, S // 16], U16, name="offsets")
+        x_rows = xT.rearrange("(p j) w -> p j w", j=PACK)
+        planes = [keep.tile([P, T], F32, name=f"plane{j}") for j in range(PACK)]
+        nc.sync.dma_start(planes[0][:], x_rows[:, 0, :])
+        nc.sync.dma_start(offsets[:], offs)
+        for j in range(1, PACK - 1):
+            nc.sync.dma_start(planes[j][:], x_rows[:, j, :])
+        c0 = 0
+        for width, engine in LAST_CHUNKS:
+            nc.sync.dma_start(planes[PACK - 1][:, c0 : c0 + width], x_rows[:, PACK - 1, c0 : c0 + width])
+            c0 = c0 + width
+        w1_rows = w1.rearrange("(p j) c -> p j c", j=PACK)
+        w1_raw = []
+        for i, (a, b) in enumerate([[0,64],[64,128]]):
+            raw = keep.tile([P, PACK, (b - a) * PACK], F32, name=f"w1_raw{i}")
+            nc.sync.dma_start(raw[:], w1_rows[:, :, a * PACK : b * PACK])
+            w1_raw.append((a, b, raw))
+
+        w2_codes = keep.tile([P, 2 * N], U8, name="w2_codes", align_bytes=64)
+        w2_plane = keep.tile([P, N], U8, name="w2_plane", align_bytes=64)
+        nc.vector.memset(w2_plane[:].bitcast(I32), 0)
+        nc.sync.dma_start(w2_codes[:].bitcast(I32), w2_words[0].bitcast(I32))
+        for q in range(4):
+            nc.sync.dma_start(w2_plane[32 * q : 32 * q + 4, :].bitcast(I32), w2_scales[0, 4 * q : 4 * q + 4, :].bitcast(I32))
+
+        sides = [keep.tile([P, V, PACK], BF16, name=f"side{s}", align_bytes=64) for s in range(2)]
+        lists = [offsets[:, s * (V // 16) : (s + 1) * (V // 16)] for s in range(2)]
+        for j in range(PACK - 1):
+            for s in range(2):
+                nc.vector.tensor_copy(sides[s][:, :, j], planes[j][:].indirect(lists[s]))
+        for s in range(2):
+            nc.vector.tensor_copy(sides[s][:, :, PACK - 1], planes[PACK - 1][:].indirect(lists[s]))
+
+        x_codes = [keep.tile([P, V], U32, name=f"x_codes{s}", align_bytes=64) for s in range(2)]
+        x_scales = [keep.tile([P, V], U8, name=f"x_scales{s}", align_bytes=64) for s in range(2)]
+        w1_codes = keep.tile([P, H], U32, name="w1_codes", align_bytes=64)
+        w1_scales = keep.tile([P, H], U8, name="w1_scales", align_bytes=64)
+
+        def quantise_x(s, cols):
+            nc.vector.quantize_mx(out=x_codes[s][:, cols].bitcast(FP8X4), scales=x_scales[s][:, cols],
+                                  in_=sides[s][:, cols, :].rearrange("p v j -> p (v j)"))
+
+        first = slice(0, 256)
+        quantise_x(0, first)
+        quantise_x(1, first)
+
+        w1_bf = keep.tile([P, PACK, P, PACK], BF16, name="w1_bf", align_bytes=64)
+        m0 = 0
+        for width, engine in W_PARTS:
+            a, b, raw = [r for r in w1_raw if r[0] <= m0 < r[1]][0]
+            dst = w1_bf[:, :, m0 : m0 + width, :].rearrange("p t m j -> p m t j")
+            src = raw[:, :, (m0 - a) * PACK : (m0 - a + width) * PACK].rearrange("p j (m t) -> p m t j", t=PACK)
+            if engine == "s":
+                nc.scalar.copy(dst, src)
+            elif engine == "g":
+                nc.gpsimd.tensor_copy(dst, src)
+            else:
+                nc.vector.tensor_copy(dst, src)
+            m0 = m0 + width
+        for t0, t1 in [[0,2],[2,4]]:
+            nc.vector.quantize_mx(out=w1_codes[:, t0 * P : t1 * P].bitcast(FP8X4), scales=w1_scales[:, t0 * P : t1 * P],
+                                  in_=w1_bf[:, t0:t1, :, :].rearrange("p t m j -> p (t m j)"))
+        for a, b in [[256,512]]:
+            quantise_x(0, slice(a, b))
+            quantise_x(1, slice(a, b))
+
+        def layer(s, cols):
+            bank = psum.tile([P, PACK, CH], F32, name="bank")
+            for t in range(PACK):
+                m = slice(t * P, (t + 1) * P)
+                nc.tensor.matmul_mx(out=bank[:, t, :], lhsT=w1_codes[:, m].bitcast(FP8X4), lhsT_scale=w1_scales[:, m],
+                                    rhs=x_codes[s][:, cols].bitcast(FP8X4), rhs_scale=x_scales[s][:, cols], start=True, stop=True)
+            return bank
+
+        banks = [(layer(0, slice(c * CH, (c + 1) * CH)), layer(1, slice(c * CH, (c + 1) * CH))) for c in range(NCH)]
+        out_rows = out.rearrange("(h p) v -> p h v", p=P)
+        for c in range(NCH):
+            cols = slice(c * CH, (c + 1) * CH)
+            bank_a, bank_b = banks[c]
+            h_a = ring.tile([P, CH, PACK], F32, name="h_a")
+            nc.scalar.activation(h_a[:], bank_a[:].rearrange("p t v -> p v t"), ACT.Relu)
+            diff = ring.tile([P, CH, PACK], BF16, name="diff", align_bytes=64)
+            nc.vector.scalar_tensor_tensor(diff[:], bank_b[:].rearrange("p t v -> p v t"), 0.0, h_a[:], ALU.max, ALU.subtract)
+            z = ring.tile([P, CH * PACK], BF16, name="z", align_bytes=64)
+            flat = diff[:].rearrange("p v t -> p (v t)")
+            if c in ABS_ON_SCALAR:
+                nc.scalar.activation(z[:], flat, ACT.Abs)
+            else:
+                nc.vector.scalar_tensor_tensor(z[:], flat, -1.0, flat, ALU.mult, ALU.max)
+            z_codes = ring.tile([P, CH], U32, name="z_codes", align_bytes=64)
+            z_scales = ring.tile([P, CH], U8, name="z_scales", align_bytes=64)
+            nc.vector.quantize_mx(out=z_codes[:].bitcast(FP8X4), scales=z_scales[:], in_=z[:])
+            acc = psum.tile([P, PACK, CH], F32, name="bank")
+            for h in range(N // P):
+                nc.tensor.matmul_mx(out=acc[:, h, :], lhsT=w2_codes[:, 2 * P * h : 2 * P * (h + 1)].bitcast(FP4X4),
+                                    lhsT_scale=w2_plane[:, P * h : P * (h + 1)],
+                                    rhs=z_codes[:].bitcast(FP8X4), rhs_scale=z_scales[:], start=True, stop=True)
+            res = ring.tile([P, N // P, CH], F32, name="res")
+            nc.scalar.copy(res[:], acc[:, 0 : N // P, :])
+            nc.sync.dma_start(out_rows[:, :, cols], res[:])

@@ -20,9 +20,9 @@ P = 128
 PACK = 4
 CH = 128
 NCH = V // CH
-ABS_ON_SCALAR = [0]
-LAST_CHUNKS = [[4096,"v"]]
-W_PARTS = [[64,"s"],[64,"s"]]
+HALF = V // 2
+M_HALF = P // 2
+M_VECTOR = 24
 
 
 def tile_picked_siam_abs_e_kernel(tc, xT, w1, w2_words, w2_scales, offs, out):
@@ -35,100 +35,121 @@ def tile_picked_siam_abs_e_kernel(tc, xT, w1, w2_words, w2_scales, offs, out):
         offsets = keep.tile([P, S // 16], U16, name="offsets")
         x_rows = xT.rearrange("(p j) w -> p j w", j=PACK)
         planes = [keep.tile([P, T], F32, name=f"plane{j}") for j in range(PACK)]
-        nc.sync.dma_start(planes[0][:], x_rows[:, 0, :])
-        nc.sync.dma_start(offsets[:], offs)
-        for j in range(1, PACK - 1):
-            nc.sync.dma_start(planes[j][:], x_rows[:, j, :])
-        c0 = 0
-        for width, engine in LAST_CHUNKS:
-            nc.sync.dma_start(planes[PACK - 1][:, c0 : c0 + width], x_rows[:, PACK - 1, c0 : c0 + width])
-            c0 = c0 + width
-        w1_rows = w1.rearrange("(p j) c -> p j c", j=PACK)
-        w1_raw = []
-        for i, (a, b) in enumerate([[0,64],[64,128]]):
-            raw = keep.tile([P, PACK, (b - a) * PACK], F32, name=f"w1_raw{i}")
-            nc.sync.dma_start(raw[:], w1_rows[:, :, a * PACK : b * PACK])
-            w1_raw.append((a, b, raw))
-
-        w2_codes = keep.tile([P, 2 * N], U8, name="w2_codes", align_bytes=64)
         w2_plane = keep.tile([P, N], U8, name="w2_plane", align_bytes=64)
         nc.vector.memset(w2_plane[:].bitcast(I32), 0)
-        nc.sync.dma_start(w2_codes[:].bitcast(I32), w2_words[0].bitcast(I32))
+        nc.sync.dma_start(planes[0][:], x_rows[:, 0, :])
+        nc.sync.dma_start(offsets[:], offs)
         for q in range(4):
             nc.sync.dma_start(w2_plane[32 * q : 32 * q + 4, :].bitcast(I32), w2_scales[0, 4 * q : 4 * q + 4, :].bitcast(I32))
+        for j in range(1, PACK):
+            nc.sync.dma_start(planes[j][:], x_rows[:, j, :])
+        w1_rows = w1.rearrange("(p j) c -> p j c", j=PACK)
+        w1_lo = keep.tile([P, PACK, H // 2], F32, name="w1_lo")
+        w1_hi = keep.tile([P, PACK, H // 2], F32, name="w1_hi", tag="late", align_bytes=64)
+        w2_codes = keep.tile([P, 2 * N], U8, name="w2_codes", align_bytes=64)
+        nc.sync.dma_start(w1_lo[:], w1_rows[:, :, : H // 2])
+        nc.sync.dma_start(w2_codes[:].bitcast(I32), w2_words[0].bitcast(I32))
+        nc.sync.dma_start(w1_hi[:], w1_rows[:, :, H // 2 :])
+
+        zeros = keep.tile([P, HALF * PACK], BF16, name="zeros", align_bytes=64)
+        nc.vector.memset(zeros[:], 0.0)
+        zero_codes = keep.tile([P, HALF], U32, name="zero_codes", align_bytes=64)
+        zero_scales = keep.tile([P, HALF], U8, name="zero_scales", align_bytes=64)
+        nc.vector.quantize_mx(out=zero_codes[:].bitcast(FP8X4), scales=zero_scales[:], in_=zeros[:])
+        idle = psum.tile([P, PACK, CH], F32, name="bank")
+        for r in range(5):
+            nc.tensor.matmul_mx(out=idle[:, 0:2, :].rearrange("p t v -> p (t v)"), lhsT=w2_codes[:, 0 : 2 * P].bitcast(FP4X4), lhsT_scale=w2_plane[:, 0:P],
+                                rhs=zero_codes[:].bitcast(FP8X4), rhs_scale=zero_scales[:], start=True, stop=True)
 
         sides = [keep.tile([P, V, PACK], BF16, name=f"side{s}", align_bytes=64) for s in range(2)]
-        lists = [offsets[:, s * (V // 16) : (s + 1) * (V // 16)] for s in range(2)]
-        for j in range(PACK - 1):
+        for j in range(PACK):
             for s in range(2):
-                nc.vector.tensor_copy(sides[s][:, :, j], planes[j][:].indirect(lists[s]))
-        for s in range(2):
-            nc.vector.tensor_copy(sides[s][:, :, PACK - 1], planes[PACK - 1][:].indirect(lists[s]))
+                nc.vector.tensor_copy(sides[s][:, :, j], planes[j][:].indirect(offsets[:, s * (V // 16) : (s + 1) * (V // 16)]))
+
+        w1_bf = keep.tile([P, PACK, P, PACK], BF16, name="w1_bf", align_bytes=64)
+
+        def deal(copy, raw, m_base, m0, m1):
+            copy(w1_bf[:, :, m_base + m0 : m_base + m1, :].rearrange("p t m j -> p m t j"),
+                 raw[:, :, m0 * PACK : m1 * PACK].rearrange("p j (m t) -> p m t j", t=PACK))
+
+        deal(nc.scalar.copy, w1_lo, 0, 0, M_HALF)
+        deal(nc.scalar.copy, w1_hi, M_HALF, 0, M_HALF - M_VECTOR)
+        deal(nc.vector.tensor_copy, w1_hi, M_HALF, M_HALF - M_VECTOR, M_HALF)
 
         x_codes = [keep.tile([P, V], U32, name=f"x_codes{s}", align_bytes=64) for s in range(2)]
-        x_scales = [keep.tile([P, V], U8, name=f"x_scales{s}", align_bytes=64) for s in range(2)]
+        first_scales = keep.tile([P, HALF], U8, name="first_scales", align_bytes=64)
+        late_scales = keep.tile([P, 3, HALF], U8, name="late_scales", tag="late", align_bytes=64)
+        x_scales = {(0, 0): first_scales[:], (1, 0): late_scales[:, 0, :], (0, 1): late_scales[:, 1, :], (1, 1): late_scales[:, 2, :]}
         w1_codes = keep.tile([P, H], U32, name="w1_codes", align_bytes=64)
         w1_scales = keep.tile([P, H], U8, name="w1_scales", align_bytes=64)
 
-        def quantise_x(s, cols):
-            nc.vector.quantize_mx(out=x_codes[s][:, cols].bitcast(FP8X4), scales=x_scales[s][:, cols],
+        def quantise_x(s, half):
+            cols = slice(half * HALF, (half + 1) * HALF)
+            nc.vector.quantize_mx(out=x_codes[s][:, cols].bitcast(FP8X4), scales=x_scales[s, half],
                                   in_=sides[s][:, cols, :].rearrange("p v j -> p (v j)"))
 
-        first = slice(0, 256)
-        quantise_x(0, first)
-        quantise_x(1, first)
-
-        w1_bf = keep.tile([P, PACK, P, PACK], BF16, name="w1_bf", align_bytes=64)
-        m0 = 0
-        for width, engine in W_PARTS:
-            a, b, raw = [r for r in w1_raw if r[0] <= m0 < r[1]][0]
-            dst = w1_bf[:, :, m0 : m0 + width, :].rearrange("p t m j -> p m t j")
-            src = raw[:, :, (m0 - a) * PACK : (m0 - a + width) * PACK].rearrange("p j (m t) -> p m t j", t=PACK)
-            if engine == "s":
-                nc.scalar.copy(dst, src)
-            elif engine == "g":
-                nc.gpsimd.tensor_copy(dst, src)
-            else:
-                nc.vector.tensor_copy(dst, src)
-            m0 = m0 + width
+        quantise_x(0, 0)
         for t0, t1 in [[0,2],[2,4]]:
             nc.vector.quantize_mx(out=w1_codes[:, t0 * P : t1 * P].bitcast(FP8X4), scales=w1_scales[:, t0 * P : t1 * P],
                                   in_=w1_bf[:, t0:t1, :, :].rearrange("p t m j -> p (t m j)"))
-        for a, b in [[256,512]]:
-            quantise_x(0, slice(a, b))
-            quantise_x(1, slice(a, b))
+        quantise_x(1, 0)
+        quantise_x(0, 1)
+        quantise_x(1, 1)
 
-        def layer(s, cols):
+        def layer(s, c):
             bank = psum.tile([P, PACK, CH], F32, name="bank")
+            half, part = divmod(c * CH, HALF)
             for t in range(PACK):
                 m = slice(t * P, (t + 1) * P)
                 nc.tensor.matmul_mx(out=bank[:, t, :], lhsT=w1_codes[:, m].bitcast(FP8X4), lhsT_scale=w1_scales[:, m],
-                                    rhs=x_codes[s][:, cols].bitcast(FP8X4), rhs_scale=x_scales[s][:, cols], start=True, stop=True)
+                                    rhs=x_codes[s][:, c * CH : (c + 1) * CH].bitcast(FP8X4),
+                                    rhs_scale=x_scales[s, half][:, part : part + CH], start=True, stop=True)
             return bank
 
-        banks = [(layer(0, slice(c * CH, (c + 1) * CH)), layer(1, slice(c * CH, (c + 1) * CH))) for c in range(NCH)]
+        banks = {}
+        for s, c in [[0,0],[0,1],[1,0],[1,1],[0,2],[0,3],[1,2],[1,3]]:
+            banks[s, c] = layer(s, c)
         out_rows = out.rearrange("(h p) v -> p h v", p=P)
-        for c in range(NCH):
-            cols = slice(c * CH, (c + 1) * CH)
-            bank_a, bank_b = banks[c]
-            h_a = ring.tile([P, CH, PACK], F32, name="h_a")
-            nc.scalar.activation(h_a[:], bank_a[:].rearrange("p t v -> p v t"), ACT.Relu)
-            diff = ring.tile([P, CH, PACK], BF16, name="diff", align_bytes=64)
-            nc.vector.scalar_tensor_tensor(diff[:], bank_b[:].rearrange("p t v -> p v t"), 0.0, h_a[:], ALU.max, ALU.subtract)
-            z = ring.tile([P, CH * PACK], BF16, name="z", align_bytes=64)
-            flat = diff[:].rearrange("p v t -> p (v t)")
-            if c in ABS_ON_SCALAR:
-                nc.scalar.activation(z[:], flat, ACT.Abs)
+        h_a = [ring.tile([P, CH, PACK], F32, name="h_a") for c in range(NCH)]
+        diff = [ring.tile([P, CH, PACK], BF16, name="diff", align_bytes=64) for c in range(NCH)]
+        z = [ring.tile([P, CH * PACK], BF16, name="z", align_bytes=64) for c in range(NCH)]
+        z_codes = [ring.tile([P, CH], U32, name="z_codes", align_bytes=64) for c in range(NCH)]
+        z_scales = [ring.tile([P, CH], U8, name="z_scales", align_bytes=64) for c in range(NCH)]
+
+        def relu(c):
+            nc.scalar.activation(h_a[c][:], banks[0, c][:].rearrange("p t v -> p v t"), ACT.Relu)
+
+        def sub(c):
+            nc.vector.scalar_tensor_tensor(diff[c][:], banks[1, c][:].rearrange("p t v -> p v t"), 0.0, h_a[c][:], ALU.max, ALU.subtract)
+
+        def mag(c, on_scalar, a, b):
+            flat = diff[c][:].rearrange("p v t -> p (v t)")[:, a:b]
+            if on_scalar:
+                nc.scalar.activation(z[c][:, a:b], flat, ACT.Abs)
             else:
-                nc.vector.scalar_tensor_tensor(z[:], flat, -1.0, flat, ALU.mult, ALU.max)
-            z_codes = ring.tile([P, CH], U32, name="z_codes", align_bytes=64)
-            z_scales = ring.tile([P, CH], U8, name="z_scales", align_bytes=64)
-            nc.vector.quantize_mx(out=z_codes[:].bitcast(FP8X4), scales=z_scales[:], in_=z[:])
+                nc.vector.scalar_tensor_tensor(z[c][:, a:b], flat, -1.0, flat, ALU.mult, ALU.max)
+
+        def project(c, on_scalar):
+            nc.vector.quantize_mx(out=z_codes[c][:].bitcast(FP8X4), scales=z_scales[c][:], in_=z[c][:])
             acc = psum.tile([P, PACK, CH], F32, name="bank")
             for h in range(N // P):
                 nc.tensor.matmul_mx(out=acc[:, h, :], lhsT=w2_codes[:, 2 * P * h : 2 * P * (h + 1)].bitcast(FP4X4),
                                     lhsT_scale=w2_plane[:, P * h : P * (h + 1)],
-                                    rhs=z_codes[:].bitcast(FP8X4), rhs_scale=z_scales[:], start=True, stop=True)
+                                    rhs=z_codes[c][:].bitcast(FP8X4), rhs_scale=z_scales[c][:], start=True, stop=True)
             res = ring.tile([P, N // P, CH], F32, name="res")
-            nc.scalar.copy(res[:], acc[:, 0 : N // P, :])
-            nc.sync.dma_start(out_rows[:, :, cols], res[:])
+            if on_scalar:
+                nc.scalar.copy(res[:], acc[:, 0 : N // P, :])
+            else:
+                nc.vector.tensor_copy(res[:], acc[:, 0 : N // P, :])
+            nc.sync.dma_start(out_rows[:, :, c * CH : (c + 1) * CH], res[:])
+
+        for c in range(NCH):
+            relu(c)
+        for c in range(NCH):
+            sub(c)
+        for c in range(NCH - 1):
+            mag(c, True, 0, 512)
+        mag(3, True, 0, 256)
+        mag(3, False, 256, 512)
+        for c in range(NCH):
+            project(c, True)

@@ -22,7 +22,7 @@ CH = 128
 NCH = V // CH
 HALF = V // 2
 M_HALF = P // 2
-M_VECTOR = 24
+PIECES = [(0, 1024), (1024, 2048), (2048, 3072), (3072, 3584), (3584, 4096)]
 
 
 def tile_picked_siam_abs_e_kernel(tc, xT, w1, w2_words, w2_scales, offs, out):
@@ -41,10 +41,12 @@ def tile_picked_siam_abs_e_kernel(tc, xT, w1, w2_words, w2_scales, offs, out):
         nc.sync.dma_start(offsets[:], offs)
         for q in range(4):
             nc.sync.dma_start(w2_plane[32 * q : 32 * q + 4, :].bitcast(I32), w2_scales[0, 4 * q : 4 * q + 4, :].bitcast(I32))
-        for j in range(1, PACK):
+        for j in range(1, PACK - 1):
             nc.sync.dma_start(planes[j][:], x_rows[:, j, :])
+        for a, b in PIECES:
+            nc.sync.dma_start(planes[PACK - 1][:, a:b], x_rows[:, PACK - 1, a:b])
         w1_rows = w1.rearrange("(p j) c -> p j c", j=PACK)
-        w1_lo = keep.tile([P, PACK, H // 2], F32, name="w1_lo")
+        w1_lo = keep.tile([P, PACK, H // 2], F32, name="w1_lo", tag="early", align_bytes=64)
         w1_hi = keep.tile([P, PACK, H // 2], F32, name="w1_hi", tag="late", align_bytes=64)
         w2_codes = keep.tile([P, 2 * N], U8, name="w2_codes", align_bytes=64)
         nc.sync.dma_start(w1_lo[:], w1_rows[:, :, : H // 2])
@@ -62,52 +64,62 @@ def tile_picked_siam_abs_e_kernel(tc, xT, w1, w2_words, w2_scales, offs, out):
                                 rhs=zero_codes[:].bitcast(FP8X4), rhs_scale=zero_scales[:], start=True, stop=True)
 
         sides = [keep.tile([P, V, PACK], BF16, name=f"side{s}", align_bytes=64) for s in range(2)]
-        for j in range(PACK):
+        lists = [offsets[:, s * (V // 16) : (s + 1) * (V // 16)] for s in range(2)]
+        for j in range(PACK - 1):
             for s in range(2):
-                nc.vector.tensor_copy(sides[s][:, :, j], planes[j][:].indirect(offsets[:, s * (V // 16) : (s + 1) * (V // 16)]))
+                nc.vector.tensor_copy(sides[s][:, :, j], planes[j][:].indirect(lists[s]))
+        last_bf = keep.tile([P, T], BF16, name="last_bf", align_bytes=64)
+        for i, (a, b) in enumerate(PIECES):
+            copy = nc.vector.tensor_copy if i == len(PIECES) - 2 else nc.scalar.copy
+            copy(last_bf[:, a:b], planes[PACK - 1][:, a:b])
+        nc.vector.tensor_copy(sides[0][:, :, PACK - 1], planes[PACK - 1][:].indirect(lists[0]))
+        nc.scalar.activation(sides[1][:, :, PACK - 1], last_bf[:].indirect(lists[1]), ACT.Copy)
 
         w1_bf = keep.tile([P, PACK, P, PACK], BF16, name="w1_bf", align_bytes=64)
 
-        def deal(copy, raw, m_base, m0, m1):
-            copy(w1_bf[:, :, m_base + m0 : m_base + m1, :].rearrange("p t m j -> p m t j"),
-                 raw[:, :, m0 * PACK : m1 * PACK].rearrange("p j (m t) -> p m t j", t=PACK))
+        def deal(copy, raw, m_base, t0, t1):
+            copy(w1_bf[:, t0:t1, m_base : m_base + M_HALF, :].rearrange("p t m j -> p m t j"),
+                 raw[:].rearrange("p j (m t) -> p m t j", t=PACK)[:, :, t0:t1, :])
 
-        deal(nc.scalar.copy, w1_lo, 0, 0, M_HALF)
-        deal(nc.scalar.copy, w1_hi, M_HALF, 0, M_HALF - M_VECTOR)
-        deal(nc.vector.tensor_copy, w1_hi, M_HALF, M_HALF - M_VECTOR, M_HALF)
+        deal(nc.vector.tensor_copy, w1_lo, 0, 0, PACK)
+        deal(nc.vector.tensor_copy, w1_hi, M_HALF, 0, PACK // 2)
+        deal(nc.scalar.copy, w1_hi, M_HALF, PACK // 2, PACK)
 
         x_codes = [keep.tile([P, V], U32, name=f"x_codes{s}", align_bytes=64) for s in range(2)]
-        first_scales = keep.tile([P, HALF], U8, name="first_scales", align_bytes=64)
-        late_scales = keep.tile([P, 3, HALF], U8, name="late_scales", tag="late", align_bytes=64)
-        x_scales = {(0, 0): first_scales[:], (1, 0): late_scales[:, 0, :], (0, 1): late_scales[:, 1, :], (1, 1): late_scales[:, 2, :]}
+        first_scales = keep.tile([P, HALF], U8, name="first_scales", tag="early", align_bytes=64)
+        late_scales = keep.tile([P, 2, V], U8, name="late_scales", tag="late", align_bytes=64)
         w1_codes = keep.tile([P, H], U32, name="w1_codes", align_bytes=64)
         w1_scales = keep.tile([P, H], U8, name="w1_scales", align_bytes=64)
 
-        def quantise_x(s, half):
-            cols = slice(half * HALF, (half + 1) * HALF)
-            nc.vector.quantize_mx(out=x_codes[s][:, cols].bitcast(FP8X4), scales=x_scales[s, half],
+        def x_scales(s, c0, c1):
+            if s == 0 and c1 <= NCH // 2:
+                return first_scales[:, c0 * CH : c1 * CH]
+            return late_scales[:, s, c0 * CH : c1 * CH]
+
+        def quantise_x(s, c0, c1):
+            cols = slice(c0 * CH, c1 * CH)
+            nc.vector.quantize_mx(out=x_codes[s][:, cols].bitcast(FP8X4), scales=x_scales(s, c0, c1),
                                   in_=sides[s][:, cols, :].rearrange("p v j -> p (v j)"))
 
-        quantise_x(0, 0)
-        for t0, t1 in [[0,2],[2,4]]:
+        quantise_x(0, 0, 2)
+        for t0, t1 in [[0, 2], [2, 4]]:
             nc.vector.quantize_mx(out=w1_codes[:, t0 * P : t1 * P].bitcast(FP8X4), scales=w1_scales[:, t0 * P : t1 * P],
                                   in_=w1_bf[:, t0:t1, :, :].rearrange("p t m j -> p (t m j)"))
-        quantise_x(1, 0)
-        quantise_x(0, 1)
-        quantise_x(1, 1)
+        quantise_x(1, 0, 2)
+        quantise_x(0, 2, 4)
+        quantise_x(1, 2, 4)
 
         def layer(s, c):
             bank = psum.tile([P, PACK, CH], F32, name="bank")
-            half, part = divmod(c * CH, HALF)
             for t in range(PACK):
                 m = slice(t * P, (t + 1) * P)
                 nc.tensor.matmul_mx(out=bank[:, t, :], lhsT=w1_codes[:, m].bitcast(FP8X4), lhsT_scale=w1_scales[:, m],
                                     rhs=x_codes[s][:, c * CH : (c + 1) * CH].bitcast(FP8X4),
-                                    rhs_scale=x_scales[s, half][:, part : part + CH], start=True, stop=True)
+                                    rhs_scale=x_scales(s, c, c + 1), start=True, stop=True)
             return bank
 
         banks = {}
-        for s, c in [[0,0],[0,1],[1,0],[1,1],[0,2],[0,3],[1,2],[1,3]]:
+        for s, c in [[0, 0], [0, 1], [1, 0], [0, 2], [1, 1], [0, 3], [1, 2], [1, 3]]:
             banks[s, c] = layer(s, c)
         out_rows = out.rearrange("(h p) v -> p h v", p=P)
         h_a = [ring.tile([P, CH, PACK], F32, name="h_a") for c in range(NCH)]
@@ -122,25 +134,37 @@ def tile_picked_siam_abs_e_kernel(tc, xT, w1, w2_words, w2_scales, offs, out):
         def sub(c):
             nc.vector.scalar_tensor_tensor(diff[c][:], banks[1, c][:].rearrange("p t v -> p v t"), 0.0, h_a[c][:], ALU.max, ALU.subtract)
 
-        def mag(c, on_scalar, a, b):
-            flat = diff[c][:].rearrange("p v t -> p (v t)")[:, a:b]
-            if on_scalar:
-                nc.scalar.activation(z[c][:, a:b], flat, ACT.Abs)
-            else:
-                nc.vector.scalar_tensor_tensor(z[c][:, a:b], flat, -1.0, flat, ALU.mult, ALU.max)
+        def flat(c):
+            return diff[c][:].rearrange("p v t -> p (v t)")
 
-        def project(c, on_scalar):
+        def mag_scalar(c, a, b):
+            nc.scalar.activation(z[c][:, a:b], flat(c)[:, a:b], ACT.Abs)
+
+        def mag_vector(c, a, b):
+            nc.vector.scalar_tensor_tensor(z[c][:, a:b], flat(c)[:, a:b], -1.0, flat(c)[:, a:b], ALU.mult, ALU.max)
+
+        def quantise_z(c):
             nc.vector.quantize_mx(out=z_codes[c][:].bitcast(FP8X4), scales=z_scales[c][:], in_=z[c][:])
+
+        def project(acc, c, h):
+            nc.tensor.matmul_mx(out=acc, lhsT=w2_codes[:, 2 * P * h : 2 * P * (h + 1)].bitcast(FP4X4),
+                                lhsT_scale=w2_plane[:, P * h : P * (h + 1)],
+                                rhs=z_codes[c][:].bitcast(FP8X4), rhs_scale=z_scales[c][:], start=True, stop=True)
+
+        def finish(c, copy):
             acc = psum.tile([P, PACK, CH], F32, name="bank")
             for h in range(N // P):
-                nc.tensor.matmul_mx(out=acc[:, h, :], lhsT=w2_codes[:, 2 * P * h : 2 * P * (h + 1)].bitcast(FP4X4),
-                                    lhsT_scale=w2_plane[:, P * h : P * (h + 1)],
-                                    rhs=z_codes[c][:].bitcast(FP8X4), rhs_scale=z_scales[c][:], start=True, stop=True)
+                project(acc[:, h, :], c, h)
             res = ring.tile([P, N // P, CH], F32, name="res")
-            if on_scalar:
-                nc.scalar.copy(res[:], acc[:, 0 : N // P, :])
-            else:
-                nc.vector.tensor_copy(res[:], acc[:, 0 : N // P, :])
+            copy(res[:], acc[:, 0 : N // P, :])
+            nc.sync.dma_start(out_rows[:, :, c * CH : (c + 1) * CH], res[:])
+
+        def finish_split(c):
+            res = ring.tile([P, N // P, CH], F32, name="res")
+            for h, copy in enumerate((nc.scalar.copy, nc.vector.tensor_copy)):
+                acc = psum.tile([P, PACK, CH], F32, name="bank")
+                project(acc[:, 0, :], c, h)
+                copy(res[:, h, :], acc[:, 0, :])
             nc.sync.dma_start(out_rows[:, :, c * CH : (c + 1) * CH], res[:])
 
         for c in range(NCH):
@@ -148,8 +172,13 @@ def tile_picked_siam_abs_e_kernel(tc, xT, w1, w2_words, w2_scales, offs, out):
         for c in range(NCH):
             sub(c)
         for c in range(NCH - 1):
-            mag(c, True, 0, 512)
-        mag(3, True, 0, 256)
-        mag(3, False, 256, 512)
-        for c in range(NCH):
-            project(c, True)
+            mag_scalar(c, 0, 512)
+        quantise_z(0)
+        mag_vector(3, 0, 512)
+        quantise_z(1)
+        quantise_z(3)
+        quantise_z(2)
+        finish(0, nc.scalar.copy)
+        finish(1, nc.scalar.copy)
+        finish(3, nc.vector.tensor_copy)
+        finish_split(2)

@@ -22,7 +22,8 @@ CH = 128
 NCH = V // CH
 HALF = V // 2
 M_HALF = P // 2
-PIECES = [(0, 1024), (1024, 2048), (2048, 3072), (3072, 3584), (3584, 4096)]
+PIECES = [(0, 2560), (2560, 3584), (3584, 4096)]
+CAST_SCALAR = 1536
 
 
 def tile_picked_siam_abs_e_kernel(tc, xT, w1, w2_words, w2_scales, offs, out):
@@ -39,8 +40,10 @@ def tile_picked_siam_abs_e_kernel(tc, xT, w1, w2_words, w2_scales, offs, out):
         nc.vector.memset(w2_plane[:].bitcast(I32), 0)
         nc.sync.dma_start(planes[0][:], x_rows[:, 0, :])
         nc.sync.dma_start(offsets[:], offs)
-        for q in range(4):
+
+        def load_scales(q):
             nc.sync.dma_start(w2_plane[32 * q : 32 * q + 4, :].bitcast(I32), w2_scales[0, 4 * q : 4 * q + 4, :].bitcast(I32))
+
         for j in range(1, PACK - 1):
             nc.sync.dma_start(planes[j][:], x_rows[:, j, :])
         for a, b in PIECES:
@@ -50,8 +53,9 @@ def tile_picked_siam_abs_e_kernel(tc, xT, w1, w2_words, w2_scales, offs, out):
         w1_hi = keep.tile([P, PACK, H // 2], F32, name="w1_hi", tag="late", align_bytes=64)
         w2_codes = keep.tile([P, 2 * N], U8, name="w2_codes", align_bytes=64)
         nc.sync.dma_start(w1_lo[:], w1_rows[:, :, : H // 2])
-        nc.sync.dma_start(w2_codes[:].bitcast(I32), w2_words[0].bitcast(I32))
+        load_scales(0)
         nc.sync.dma_start(w1_hi[:], w1_rows[:, :, H // 2 :])
+        nc.sync.dma_start(w2_codes[:].bitcast(I32), w2_words[0].bitcast(I32))
 
         zeros = keep.tile([P, HALF * PACK], BF16, name="zeros", align_bytes=64)
         nc.vector.memset(zeros[:], 0.0)
@@ -60,8 +64,10 @@ def tile_picked_siam_abs_e_kernel(tc, xT, w1, w2_words, w2_scales, offs, out):
         nc.vector.quantize_mx(out=zero_codes[:].bitcast(FP8X4), scales=zero_scales[:], in_=zeros[:])
         idle = psum.tile([P, PACK, CH], F32, name="bank")
         for r in range(5):
-            nc.tensor.matmul_mx(out=idle[:, 0:2, :].rearrange("p t v -> p (t v)"), lhsT=w2_codes[:, 0 : 2 * P].bitcast(FP4X4), lhsT_scale=w2_plane[:, 0:P],
+            nc.tensor.matmul_mx(out=idle[:, 0:2, :].rearrange("p t v -> p (t v)"), lhsT=zero_codes[:, 0:P].bitcast(FP8X4), lhsT_scale=w2_plane[:, 0:P],
                                 rhs=zero_codes[:].bitcast(FP8X4), rhs_scale=zero_scales[:], start=True, stop=True)
+        for q in range(1, 4):
+            load_scales(q)
 
         sides = [keep.tile([P, V, PACK], BF16, name=f"side{s}", align_bytes=64) for s in range(2)]
         lists = [offsets[:, s * (V // 16) : (s + 1) * (V // 16)] for s in range(2)]
@@ -69,8 +75,8 @@ def tile_picked_siam_abs_e_kernel(tc, xT, w1, w2_words, w2_scales, offs, out):
             for s in range(2):
                 nc.vector.tensor_copy(sides[s][:, :, j], planes[j][:].indirect(lists[s]))
         last_bf = keep.tile([P, T], BF16, name="last_bf", align_bytes=64)
-        for i, (a, b) in enumerate(PIECES):
-            copy = nc.vector.tensor_copy if i == len(PIECES) - 2 else nc.scalar.copy
+        for copy, a, b in ((nc.scalar.copy, 0, CAST_SCALAR), (nc.vector.tensor_copy, CAST_SCALAR, PIECES[0][1]),
+                           (nc.vector.tensor_copy, *PIECES[1]), (nc.scalar.copy, *PIECES[2])):
             copy(last_bf[:, a:b], planes[PACK - 1][:, a:b])
         nc.vector.tensor_copy(sides[0][:, :, PACK - 1], planes[PACK - 1][:].indirect(lists[0]))
         nc.scalar.activation(sides[1][:, :, PACK - 1], last_bf[:].indirect(lists[1]), ACT.Copy)
@@ -160,12 +166,12 @@ def tile_picked_siam_abs_e_kernel(tc, xT, w1, w2_words, w2_scales, offs, out):
             nc.sync.dma_start(out_rows[:, :, c * CH : (c + 1) * CH], res[:])
 
         def finish_split(c):
-            res = ring.tile([P, N // P, CH], F32, name="res")
-            for h, copy in enumerate((nc.scalar.copy, nc.vector.tensor_copy)):
+            for h, (copy, queue) in enumerate(((nc.vector.tensor_copy, nc.sync), (nc.scalar.copy, nc.scalar))):
                 acc = psum.tile([P, PACK, CH], F32, name="bank")
                 project(acc[:, 0, :], c, h)
-                copy(res[:, h, :], acc[:, 0, :])
-            nc.sync.dma_start(out_rows[:, :, c * CH : (c + 1) * CH], res[:])
+                part = keep.tile([P, CH], F32, name=f"part{h}")
+                copy(part[:], acc[:, 0, :])
+                queue.dma_start(out_rows[:, h, c * CH : (c + 1) * CH], part[:])
 
         for c in range(NCH):
             relu(c)
@@ -179,6 +185,6 @@ def tile_picked_siam_abs_e_kernel(tc, xT, w1, w2_words, w2_scales, offs, out):
         quantise_z(3)
         quantise_z(2)
         finish(0, nc.scalar.copy)
-        finish(1, nc.scalar.copy)
-        finish(3, nc.vector.tensor_copy)
+        finish(1, nc.vector.tensor_copy)
+        finish(3, nc.scalar.copy)
         finish_split(2)

@@ -24,6 +24,7 @@ HALF = V // 2
 M_HALF = P // 2
 PIECES = [(0, 2560), (2560, 3584), (3584, 4096)]
 CAST_SCALAR = 1536
+MAG_SCALAR = 320
 
 
 def tile_picked_siam_abs_e_kernel(tc, xT, w1, w2_words, w2_scales, offs, out):
@@ -57,15 +58,15 @@ def tile_picked_siam_abs_e_kernel(tc, xT, w1, w2_words, w2_scales, offs, out):
         nc.sync.dma_start(w1_hi[:], w1_rows[:, :, H // 2 :])
         nc.sync.dma_start(w2_codes[:].bitcast(I32), w2_words[0].bitcast(I32))
 
-        zeros = keep.tile([P, HALF * PACK], BF16, name="zeros", align_bytes=64)
+        zeros = keep.tile([P, V * PACK], BF16, name="zeros", align_bytes=64)
         nc.vector.memset(zeros[:], 0.0)
-        zero_codes = keep.tile([P, HALF], U32, name="zero_codes", align_bytes=64)
-        zero_scales = keep.tile([P, HALF], U8, name="zero_scales", align_bytes=64)
+        zero_codes = keep.tile([P, V], U32, name="zero_codes", align_bytes=64)
+        zero_scales = keep.tile([P, V], U8, name="zero_scales", align_bytes=64)
         nc.vector.quantize_mx(out=zero_codes[:].bitcast(FP8X4), scales=zero_scales[:], in_=zeros[:])
         idle = psum.tile([P, PACK, CH], F32, name="bank")
-        for r in range(5):
-            nc.tensor.matmul_mx(out=idle[:, 0:2, :].rearrange("p t v -> p (t v)"), lhsT=zero_codes[:, 0:P].bitcast(FP8X4), lhsT_scale=w2_plane[:, 0:P],
-                                rhs=zero_codes[:].bitcast(FP8X4), rhs_scale=zero_scales[:], start=True, stop=True)
+        for width in (V, V, HALF):
+            nc.tensor.matmul_mx(out=idle[:].rearrange("p t v -> p (t v)")[:, 0:width], lhsT=zero_codes[:, 0:P].bitcast(FP8X4), lhsT_scale=w2_plane[:, 0:P],
+                                rhs=zero_codes[:, 0:width].bitcast(FP8X4), rhs_scale=zero_scales[:, 0:width], start=True, stop=True)
         for q in range(1, 4):
             load_scales(q)
 
@@ -111,8 +112,8 @@ def tile_picked_siam_abs_e_kernel(tc, xT, w1, w2_words, w2_scales, offs, out):
         for t0, t1 in [[0, 2], [2, 4]]:
             nc.vector.quantize_mx(out=w1_codes[:, t0 * P : t1 * P].bitcast(FP8X4), scales=w1_scales[:, t0 * P : t1 * P],
                                   in_=w1_bf[:, t0:t1, :, :].rearrange("p t m j -> p (t m j)"))
-        quantise_x(1, 0, 2)
         quantise_x(0, 2, 4)
+        quantise_x(1, 0, 2)
         quantise_x(1, 2, 4)
 
         def layer(s, c):
@@ -125,7 +126,7 @@ def tile_picked_siam_abs_e_kernel(tc, xT, w1, w2_words, w2_scales, offs, out):
             return bank
 
         banks = {}
-        for s, c in [[0, 0], [0, 1], [1, 0], [0, 2], [1, 1], [0, 3], [1, 2], [1, 3]]:
+        for s, c in [[0, 0], [0, 1], [0, 2], [1, 0], [0, 3], [1, 1], [1, 2], [1, 3]]:
             banks[s, c] = layer(s, c)
         out_rows = out.rearrange("(h p) v -> p h v", p=P)
         h_a = [ring.tile([P, CH, PACK], F32, name="h_a") for c in range(NCH)]
@@ -135,7 +136,11 @@ def tile_picked_siam_abs_e_kernel(tc, xT, w1, w2_words, w2_scales, offs, out):
         z_scales = [ring.tile([P, CH], U8, name="z_scales", align_bytes=64) for c in range(NCH)]
 
         def relu(c):
-            nc.scalar.activation(h_a[c][:], banks[0, c][:].rearrange("p t v -> p v t"), ACT.Relu)
+            sums = banks[0, c][:].rearrange("p t v -> p v t")
+            if c == 1:
+                nc.vector.tensor_scalar(h_a[c][:], sums, 0.0, None, ALU.max)
+            else:
+                nc.scalar.activation(h_a[c][:], sums, ACT.Relu)
 
         def sub(c):
             nc.vector.scalar_tensor_tensor(diff[c][:], banks[1, c][:].rearrange("p t v -> p v t"), 0.0, h_a[c][:], ALU.max, ALU.subtract)
@@ -145,9 +150,6 @@ def tile_picked_siam_abs_e_kernel(tc, xT, w1, w2_words, w2_scales, offs, out):
 
         def mag_scalar(c, a, b):
             nc.scalar.activation(z[c][:, a:b], flat(c)[:, a:b], ACT.Abs)
-
-        def mag_vector(c, a, b):
-            nc.vector.scalar_tensor_tensor(z[c][:, a:b], flat(c)[:, a:b], -1.0, flat(c)[:, a:b], ALU.mult, ALU.max)
 
         def quantise_z(c):
             nc.vector.quantize_mx(out=z_codes[c][:].bitcast(FP8X4), scales=z_scales[c][:], in_=z[c][:])
@@ -177,14 +179,16 @@ def tile_picked_siam_abs_e_kernel(tc, xT, w1, w2_words, w2_scales, offs, out):
             relu(c)
         for c in range(NCH):
             sub(c)
-        for c in range(NCH - 1):
-            mag_scalar(c, 0, 512)
+        last = NCH - 1
+        for c in range(last):
+            mag_scalar(c, 0, CH * PACK)
+        mag_scalar(last, 0, MAG_SCALAR)
         quantise_z(0)
-        mag_vector(3, 0, 512)
-        quantise_z(1)
-        quantise_z(3)
-        quantise_z(2)
+        rest = flat(last)[:, MAG_SCALAR:]
+        nc.vector.scalar_tensor_tensor(z[last][:, MAG_SCALAR:], rest, -1.0, rest, ALU.mult, ALU.max)
+        for c in range(1, NCH):
+            quantise_z(c)
         finish(0, nc.scalar.copy)
         finish(1, nc.vector.tensor_copy)
-        finish(3, nc.scalar.copy)
-        finish_split(2)
+        finish(2, nc.scalar.copy)
+        finish_split(3)

@@ -50,11 +50,10 @@ def tile_picked_siam_abs_e_kernel(tc, xT, w1, w2_words, w2_scales, offs, out):
         for a, b in PIECES:
             nc.sync.dma_start(planes[PACK - 1][:, a:b], x_rows[:, PACK - 1, a:b])
         w1_rows = w1.rearrange("(p j) c -> p j c", j=PACK)
-        w1_lo = keep.tile([P, PACK, H // 2], F32, name="w1_lo", tag="early", align_bytes=64)
+        w1_lo = keep.tile([P, PACK, H // 2], F32, name="w1_lo")
         w1_hi = keep.tile([P, PACK, H // 2], F32, name="w1_hi", tag="late", align_bytes=64)
         w2_codes = keep.tile([P, 2 * N], U8, name="w2_codes", align_bytes=64)
         nc.sync.dma_start(w1_lo[:], w1_rows[:, :, : H // 2])
-        load_scales(0)
         nc.sync.dma_start(w1_hi[:], w1_rows[:, :, H // 2 :])
         nc.sync.dma_start(w2_codes[:].bitcast(I32), w2_words[0].bitcast(I32))
 
@@ -63,11 +62,7 @@ def tile_picked_siam_abs_e_kernel(tc, xT, w1, w2_words, w2_scales, offs, out):
         zero_codes = keep.tile([P, V], U32, name="zero_codes", align_bytes=64)
         zero_scales = keep.tile([P, V], U8, name="zero_scales", align_bytes=64)
         nc.vector.quantize_mx(out=zero_codes[:].bitcast(FP8X4), scales=zero_scales[:], in_=zeros[:])
-        idle = psum.tile([P, PACK, CH], F32, name="bank")
-        for width in (V, V, HALF):
-            nc.tensor.matmul_mx(out=idle[:].rearrange("p t v -> p (t v)")[:, 0:width], lhsT=zero_codes[:, 0:P].bitcast(FP8X4), lhsT_scale=w2_plane[:, 0:P],
-                                rhs=zero_codes[:, 0:width].bitcast(FP8X4), rhs_scale=zero_scales[:, 0:width], start=True, stop=True)
-        for q in range(1, 4):
+        for q in range(4):
             load_scales(q)
 
         sides = [keep.tile([P, V, PACK], BF16, name=f"side{s}", align_bytes=64) for s in range(2)]
@@ -93,7 +88,7 @@ def tile_picked_siam_abs_e_kernel(tc, xT, w1, w2_words, w2_scales, offs, out):
         deal(nc.scalar.copy, w1_hi, M_HALF, PACK // 2, PACK)
 
         x_codes = [keep.tile([P, V], U32, name=f"x_codes{s}", align_bytes=64) for s in range(2)]
-        first_scales = keep.tile([P, HALF], U8, name="first_scales", tag="early", align_bytes=64)
+        first_scales = keep.tile([P, HALF], U8, name="first_scales", align_bytes=64)
         late_scales = keep.tile([P, 2, V], U8, name="late_scales", tag="late", align_bytes=64)
         w1_codes = keep.tile([P, H], U32, name="w1_codes", align_bytes=64)
         w1_scales = keep.tile([P, H], U8, name="w1_scales", align_bytes=64)
@@ -109,6 +104,11 @@ def tile_picked_siam_abs_e_kernel(tc, xT, w1, w2_words, w2_scales, offs, out):
                                   in_=sides[s][:, cols, :].rearrange("p v j -> p (v j)"))
 
         quantise_x(0, 0, 2)
+        idle = psum.tile([P, PACK, CH], F32, name="bank")
+        for width in (V, V, HALF):
+            nc.tensor.matmul_mx(out=idle[:].rearrange("p t v -> p (t v)")[:, 0:width],
+                                lhsT=x_codes[0][:, 0:P].bitcast(FP8X4), lhsT_scale=first_scales[:, 0:P],
+                                rhs=zero_codes[:, 0:width].bitcast(FP8X4), rhs_scale=zero_scales[:, 0:width], start=True, stop=True)
         for t0, t1 in [[0, 2], [2, 4]]:
             nc.vector.quantize_mx(out=w1_codes[:, t0 * P : t1 * P].bitcast(FP8X4), scales=w1_scales[:, t0 * P : t1 * P],
                                   in_=w1_bf[:, t0:t1, :, :].rearrange("p t m j -> p (t m j)"))

@@ -22,8 +22,7 @@ CH = 128
 NCH = V // CH
 HALF = V // 2
 M_HALF = P // 2
-PIECES = [(0, 2560), (2560, 3584), (3584, 4096)]
-CAST_SCALAR = 1536
+PIECES = [(0, 1024), (1024, 2048), (2048, 3072), (3072, 3584), (3584, 4096)]
 MAG_SCALAR = 320
 
 
@@ -71,8 +70,8 @@ def tile_picked_siam_abs_e_kernel(tc, xT, w1, w2_words, w2_scales, offs, out):
             for s in range(2):
                 nc.vector.tensor_copy(sides[s][:, :, j], planes[j][:].indirect(lists[s]))
         last_bf = keep.tile([P, T], BF16, name="last_bf", align_bytes=64)
-        for copy, a, b in ((nc.scalar.copy, 0, CAST_SCALAR), (nc.vector.tensor_copy, CAST_SCALAR, PIECES[0][1]),
-                           (nc.vector.tensor_copy, *PIECES[1]), (nc.scalar.copy, *PIECES[2])):
+        for i, (a, b) in enumerate(PIECES):
+            copy = nc.vector.tensor_copy if i == len(PIECES) - 2 else nc.scalar.copy
             copy(last_bf[:, a:b], planes[PACK - 1][:, a:b])
         nc.vector.tensor_copy(sides[0][:, :, PACK - 1], planes[PACK - 1][:].indirect(lists[0]))
         nc.scalar.activation(sides[1][:, :, PACK - 1], last_bf[:].indirect(lists[1]), ACT.Copy)
@@ -103,7 +102,8 @@ def tile_picked_siam_abs_e_kernel(tc, xT, w1, w2_words, w2_scales, offs, out):
             nc.vector.quantize_mx(out=x_codes[s][:, cols].bitcast(FP8X4), scales=x_scales(s, c0, c1),
                                   in_=sides[s][:, cols, :].rearrange("p v j -> p (v j)"))
 
-        quantise_x(0, 0, 2)
+        quantise_x(0, 0, 1)
+        quantise_x(0, 1, 2)
         idle = psum.tile([P, PACK, CH], F32, name="bank")
         for width in (V, V, HALF):
             nc.tensor.matmul_mx(out=idle[:].rearrange("p t v -> p (t v)")[:, 0:width],
@@ -189,6 +189,6 @@ def tile_picked_siam_abs_e_kernel(tc, xT, w1, w2_words, w2_scales, offs, out):
         for c in range(1, NCH):
             quantise_z(c)
         finish(0, nc.scalar.copy)
-        finish(1, nc.vector.tensor_copy)
-        finish(2, nc.scalar.copy)
+        finish(1, nc.scalar.copy)
+        finish(2, nc.vector.tensor_copy)
         finish_split(3)

@@ -79,8 +79,8 @@ def tile_picked_siam_abs_e_kernel(tc, xT, w1, w2_words, w2_scales, offs, out):
         w1_bf = keep.tile([P, PACK, P, PACK], BF16, name="w1_bf", align_bytes=64)
 
         def deal(copy, raw, m_base, t0, t1):
-            copy(w1_bf[:, t0:t1, m_base : m_base + M_HALF, :].rearrange("p t m j -> p m t j"),
-                 raw[:].rearrange("p j (m t) -> p m t j", t=PACK)[:, :, t0:t1, :])
+            copy(w1_bf[:, t0:t1, m_base : m_base + M_HALF, :].rearrange("p t m j -> p m j t"),
+                 raw[:].rearrange("p j (m t) -> p m j t", t=PACK)[:, :, :, t0:t1])
 
         deal(nc.vector.tensor_copy, w1_lo, 0, 0, PACK)
         deal(nc.vector.tensor_copy, w1_hi, M_HALF, 0, PACK // 2)

@@ -22,8 +22,11 @@ CH = 128
 NCH = V // CH
 HALF = V // 2
 M_HALF = P // 2
-PIECES = [(0, 1024), (1024, 2048), (2048, 3072), (3072, 3584), (3584, 4096)]
+PIECES = [(0, 1024), (1024, 2048), (2048, 3072), (3072, 3840), (3840, 4096)]
+VECTOR_CASTS = [(2048, 3072), (3072, 3584)]
+SCALAR_CASTS = [(0, 1024), (1024, 2048), (3584, 3840), (3840, 4096)]
 MAG_SCALAR = 320
+WARM_PASSES = 4
 
 
 def tile_picked_siam_abs_e_kernel(tc, xT, w1, w2_words, w2_scales, offs, out):
@@ -56,11 +59,6 @@ def tile_picked_siam_abs_e_kernel(tc, xT, w1, w2_words, w2_scales, offs, out):
         nc.sync.dma_start(w1_hi[:], w1_rows[:, :, H // 2 :])
         nc.sync.dma_start(w2_codes[:].bitcast(I32), w2_words[0].bitcast(I32))
 
-        zeros = keep.tile([P, V * PACK], BF16, name="zeros", align_bytes=64)
-        nc.vector.memset(zeros[:], 0.0)
-        zero_codes = keep.tile([P, V], U32, name="zero_codes", align_bytes=64)
-        zero_scales = keep.tile([P, V], U8, name="zero_scales", align_bytes=64)
-        nc.vector.quantize_mx(out=zero_codes[:].bitcast(FP8X4), scales=zero_scales[:], in_=zeros[:])
         for q in range(4):
             load_scales(q)
 
@@ -70,9 +68,10 @@ def tile_picked_siam_abs_e_kernel(tc, xT, w1, w2_words, w2_scales, offs, out):
             for s in range(2):
                 nc.vector.tensor_copy(sides[s][:, :, j], planes[j][:].indirect(lists[s]))
         last_bf = keep.tile([P, T], BF16, name="last_bf", align_bytes=64)
-        for i, (a, b) in enumerate(PIECES):
-            copy = nc.vector.tensor_copy if i == len(PIECES) - 2 else nc.scalar.copy
-            copy(last_bf[:, a:b], planes[PACK - 1][:, a:b])
+        for a, b in VECTOR_CASTS:
+            nc.vector.tensor_copy(last_bf[:, a:b], planes[PACK - 1][:, a:b])
+        for a, b in SCALAR_CASTS:
+            nc.scalar.copy(last_bf[:, a:b], planes[PACK - 1][:, a:b])
         nc.vector.tensor_copy(sides[0][:, :, PACK - 1], planes[PACK - 1][:].indirect(lists[0]))
         nc.scalar.activation(sides[1][:, :, PACK - 1], last_bf[:].indirect(lists[1]), ACT.Copy)
 
@@ -82,9 +81,10 @@ def tile_picked_siam_abs_e_kernel(tc, xT, w1, w2_words, w2_scales, offs, out):
             copy(w1_bf[:, t0:t1, m_base : m_base + M_HALF, :].rearrange("p t m j -> p m j t"),
                  raw[:].rearrange("p j (m t) -> p m j t", t=PACK)[:, :, :, t0:t1])
 
-        deal(nc.vector.tensor_copy, w1_lo, 0, 0, PACK)
+        deal(nc.vector.tensor_copy, w1_lo, 0, 0, PACK // 2)
+        deal(nc.scalar.copy, w1_lo, 0, PACK // 2, PACK)
         deal(nc.vector.tensor_copy, w1_hi, M_HALF, 0, PACK // 2)
-        deal(nc.scalar.copy, w1_hi, M_HALF, PACK // 2, PACK)
+        deal(nc.vector.tensor_copy, w1_hi, M_HALF, PACK // 2, PACK)
 
         x_codes = [keep.tile([P, V], U32, name=f"x_codes{s}", align_bytes=64) for s in range(2)]
         first_scales = keep.tile([P, HALF], U8, name="first_scales", align_bytes=64)
@@ -102,13 +102,12 @@ def tile_picked_siam_abs_e_kernel(tc, xT, w1, w2_words, w2_scales, offs, out):
             nc.vector.quantize_mx(out=x_codes[s][:, cols].bitcast(FP8X4), scales=x_scales(s, c0, c1),
                                   in_=sides[s][:, cols, :].rearrange("p v j -> p (v j)"))
 
-        quantise_x(0, 0, 1)
-        quantise_x(0, 1, 2)
+        quantise_x(0, 0, 2)
         idle = psum.tile([P, PACK, CH], F32, name="bank")
-        for width in (V, V, HALF):
-            nc.tensor.matmul_mx(out=idle[:].rearrange("p t v -> p (t v)")[:, 0:width],
+        for i in range(WARM_PASSES):
+            nc.tensor.matmul_mx(out=idle[:].rearrange("p t v -> p (t v)")[:, 0:HALF],
                                 lhsT=x_codes[0][:, 0:P].bitcast(FP8X4), lhsT_scale=first_scales[:, 0:P],
-                                rhs=zero_codes[:, 0:width].bitcast(FP8X4), rhs_scale=zero_scales[:, 0:width], start=True, stop=True)
+                                rhs=x_codes[0][:, 0:HALF].bitcast(FP8X4), rhs_scale=first_scales[:, 0:HALF], start=True, stop=True)
         for t0, t1 in [[0, 2], [2, 4]]:
             nc.vector.quantize_mx(out=w1_codes[:, t0 * P : t1 * P].bitcast(FP8X4), scales=w1_scales[:, t0 * P : t1 * P],
                                   in_=w1_bf[:, t0:t1, :, :].rearrange("p t m j -> p (t m j)"))

@@ -26,7 +26,6 @@ PIECES = [(0, 1024), (1024, 2048), (2048, 3072), (3072, 3840), (3840, 4096)]
 VECTOR_CASTS = [(2048, 3072), (3072, 3584)]
 SCALAR_CASTS = [(0, 1024), (1024, 2048), (3584, 3840), (3840, 4096)]
 MAG_SCALAR = 320
-WARM_PASSES = 4
 
 
 def tile_picked_siam_abs_e_kernel(tc, xT, w1, w2_words, w2_scales, offs, out):
@@ -56,11 +55,10 @@ def tile_picked_siam_abs_e_kernel(tc, xT, w1, w2_words, w2_scales, offs, out):
         w1_hi = keep.tile([P, PACK, H // 2], F32, name="w1_hi", tag="late", align_bytes=64)
         w2_codes = keep.tile([P, 2 * N], U8, name="w2_codes", align_bytes=64)
         nc.sync.dma_start(w1_lo[:], w1_rows[:, :, : H // 2])
+        load_scales(0)
         nc.sync.dma_start(w1_hi[:], w1_rows[:, :, H // 2 :])
         nc.sync.dma_start(w2_codes[:].bitcast(I32), w2_words[0].bitcast(I32))
 
-        for q in range(4):
-            load_scales(q)
 
         sides = [keep.tile([P, V, PACK], BF16, name=f"side{s}", align_bytes=64) for s in range(2)]
         lists = [offsets[:, s * (V // 16) : (s + 1) * (V // 16)] for s in range(2)]
@@ -86,8 +84,10 @@ def tile_picked_siam_abs_e_kernel(tc, xT, w1, w2_words, w2_scales, offs, out):
         deal(nc.vector.tensor_copy, w1_hi, M_HALF, 0, PACK // 2)
         deal(nc.vector.tensor_copy, w1_hi, M_HALF, PACK // 2, PACK)
 
-        x_codes = [keep.tile([P, V], U32, name=f"x_codes{s}", align_bytes=64) for s in range(2)]
-        first_scales = keep.tile([P, HALF], U8, name="first_scales", align_bytes=64)
+        lead_codes = keep.tile([P, HALF + V], U32, name="lead_codes", align_bytes=64)
+        lead_scales = keep.tile([P, V], U8, name="lead_scales", align_bytes=64)
+        x_codes = [lead_codes[:, HALF:], keep.tile([P, V], U32, name="x_codes1", align_bytes=64)[:]]
+        first_scales = lead_scales[:, HALF:]
         late_scales = keep.tile([P, 2, V], U8, name="late_scales", tag="late", align_bytes=64)
         w1_codes = keep.tile([P, H], U32, name="w1_codes", align_bytes=64)
         w1_scales = keep.tile([P, H], U8, name="w1_scales", align_bytes=64)
@@ -103,11 +103,14 @@ def tile_picked_siam_abs_e_kernel(tc, xT, w1, w2_words, w2_scales, offs, out):
                                   in_=sides[s][:, cols, :].rearrange("p v j -> p (v j)"))
 
         quantise_x(0, 0, 2)
+        nc.vector.quantize_mx(out=lead_codes[:, :HALF].bitcast(FP8X4), scales=lead_scales[:, :HALF], in_=last_bf[:, : PACK * HALF])
         idle = psum.tile([P, PACK, CH], F32, name="bank")
-        for i in range(WARM_PASSES):
-            nc.tensor.matmul_mx(out=idle[:].rearrange("p t v -> p (t v)")[:, 0:HALF],
-                                lhsT=x_codes[0][:, 0:P].bitcast(FP8X4), lhsT_scale=first_scales[:, 0:P],
-                                rhs=x_codes[0][:, 0:HALF].bitcast(FP8X4), rhs_scale=first_scales[:, 0:HALF], start=True, stop=True)
+        for width in (HALF, HALF, HALF, V):
+            nc.tensor.matmul_mx(out=idle[:].rearrange("p t v -> p (t v)")[:, 0:width],
+                                lhsT=lead_codes[:, 0:P].bitcast(FP8X4), lhsT_scale=w2_plane[:, 0:P],
+                                rhs=lead_codes[:, 0:width].bitcast(FP8X4), rhs_scale=lead_scales[:, 0:width], start=True, stop=True)
+        for q in range(1, 4):
+            load_scales(q)
         for t0, t1 in [[0, 2], [2, 4]]:
             nc.vector.quantize_mx(out=w1_codes[:, t0 * P : t1 * P].bitcast(FP8X4), scales=w1_scales[:, t0 * P : t1 * P],
                                   in_=w1_bf[:, t0:t1, :, :].rearrange("p t m j -> p (t m j)"))

@@ -18,13 +18,23 @@ ALU = mybir.AluOpType
 
 P = 128
 PACK = 4
+LIST_GROUP = 16
+QUADRANT = 32
+SCALE_ROWS = 4
+BANKS = 8
 CH = 128
 NCH = V // CH
-HALF = V // 2
 M_HALF = P // 2
-PIECES = [(0, 1024), (1024, 2048), (2048, 3072), (3072, 3840), (3840, 4096)]
+
+LAST_PIECE = T - 256
+PIECES = [(0, 1024), (1024, 2048), (2048, 3072), (3072, LAST_PIECE), (LAST_PIECE, T)]
 VECTOR_CASTS = [(2048, 3072), (3072, 3584)]
-SCALAR_CASTS = [(0, 1024), (1024, 2048), (3584, 3840), (3840, 4096)]
+SCALAR_CASTS = [(0, 1024), (1024, 2048), (3584, LAST_PIECE), (LAST_PIECE, T)]
+EARLY_CHUNKS = 2
+EARLY = EARLY_CHUNKS * CH
+WARM = 256
+SIDE_LEAD = 3
+VECTOR_RELU = 1
 MAG_SCALAR = 320
 
 
@@ -33,68 +43,67 @@ def tile_picked_siam_abs_e_kernel(tc, xT, w1, w2_words, w2_scales, offs, out):
     with ExitStack() as ctx:
         keep = ctx.enter_context(tc.tile_pool(name="keep", bufs=1))
         ring = ctx.enter_context(tc.tile_pool(name="ring", bufs=NCH))
-        psum = ctx.enter_context(tc.psum_pool(name="psum", bufs=8))
+        psum = ctx.enter_context(tc.psum_pool(name="psum", bufs=BANKS))
 
-        offsets = keep.tile([P, S // 16], U16, name="offsets")
+        offsets = keep.tile([P, S // LIST_GROUP], U16, name="offsets")
         x_rows = xT.rearrange("(p j) w -> p j w", j=PACK)
         planes = [keep.tile([P, T], F32, name=f"plane{j}") for j in range(PACK)]
-        w2_plane = keep.tile([P, N], U8, name="w2_plane", align_bytes=64)
-        nc.vector.memset(w2_plane[:].bitcast(I32), 0)
+        last_plane = planes[PACK - 1]
+        w2_scale_rows = keep.tile([P, N], U8, name="w2_scale_rows", align_bytes=64)
+        nc.vector.memset(w2_scale_rows[:].bitcast(I32), 0)
         nc.sync.dma_start(planes[0][:], x_rows[:, 0, :])
         nc.sync.dma_start(offsets[:], offs)
-
-        def load_scales(q):
-            nc.sync.dma_start(w2_plane[32 * q : 32 * q + 4, :].bitcast(I32), w2_scales[0, 4 * q : 4 * q + 4, :].bitcast(I32))
-
         for j in range(1, PACK - 1):
             nc.sync.dma_start(planes[j][:], x_rows[:, j, :])
         for a, b in PIECES:
-            nc.sync.dma_start(planes[PACK - 1][:, a:b], x_rows[:, PACK - 1, a:b])
+            nc.sync.dma_start(last_plane[:, a:b], x_rows[:, PACK - 1, a:b])
         w1_rows = w1.rearrange("(p j) c -> p j c", j=PACK)
-        w1_lo = keep.tile([P, PACK, H // 2], F32, name="w1_lo")
-        w1_hi = keep.tile([P, PACK, H // 2], F32, name="w1_hi", tag="late", align_bytes=64)
+        w1_early = keep.tile([P, PACK, H // 2], F32, name="w1_early")
+        w1_late = keep.tile([P, PACK, H // 2], F32, name="w1_late", tag="late", align_bytes=64)
         w2_codes = keep.tile([P, 2 * N], U8, name="w2_codes", align_bytes=64)
-        nc.sync.dma_start(w1_lo[:], w1_rows[:, :, : H // 2])
-        load_scales(0)
-        nc.sync.dma_start(w1_hi[:], w1_rows[:, :, H // 2 :])
+        nc.sync.dma_start(w1_early[:], w1_rows[:, :, : H // 2])
+        nc.sync.dma_start(w1_late[:], w1_rows[:, :, H // 2 :])
         nc.sync.dma_start(w2_codes[:].bitcast(I32), w2_words[0].bitcast(I32))
-
+        for q in range(P // QUADRANT):
+            nc.sync.dma_start(w2_scale_rows[QUADRANT * q : QUADRANT * q + SCALE_ROWS, :].bitcast(I32),
+                              w2_scales[0, SCALE_ROWS * q : SCALE_ROWS * (q + 1), :].bitcast(I32))
 
         sides = [keep.tile([P, V, PACK], BF16, name=f"side{s}", align_bytes=64) for s in range(2)]
-        lists = [offsets[:, s * (V // 16) : (s + 1) * (V // 16)] for s in range(2)]
+        lists = [offsets[:, s * (V // LIST_GROUP) : (s + 1) * (V // LIST_GROUP)] for s in range(2)]
         for j in range(PACK - 1):
             for s in range(2):
                 nc.vector.tensor_copy(sides[s][:, :, j], planes[j][:].indirect(lists[s]))
         last_bf = keep.tile([P, T], BF16, name="last_bf", align_bytes=64)
         for a, b in VECTOR_CASTS:
-            nc.vector.tensor_copy(last_bf[:, a:b], planes[PACK - 1][:, a:b])
+            nc.vector.tensor_copy(last_bf[:, a:b], last_plane[:, a:b])
         for a, b in SCALAR_CASTS:
-            nc.scalar.copy(last_bf[:, a:b], planes[PACK - 1][:, a:b])
-        nc.vector.tensor_copy(sides[0][:, :, PACK - 1], planes[PACK - 1][:].indirect(lists[0]))
+            nc.scalar.copy(last_bf[:, a:b], last_plane[:, a:b])
+        nc.vector.tensor_copy(sides[0][:, :, PACK - 1], last_plane[:].indirect(lists[0]))
         nc.scalar.activation(sides[1][:, :, PACK - 1], last_bf[:].indirect(lists[1]), ACT.Copy)
 
         w1_bf = keep.tile([P, PACK, P, PACK], BF16, name="w1_bf", align_bytes=64)
+        tile_pairs = [(0, PACK // 2), (PACK // 2, PACK)]
 
         def deal(copy, raw, m_base, t0, t1):
             copy(w1_bf[:, t0:t1, m_base : m_base + M_HALF, :].rearrange("p t m j -> p m j t"),
                  raw[:].rearrange("p j (m t) -> p m j t", t=PACK)[:, :, :, t0:t1])
 
-        deal(nc.vector.tensor_copy, w1_lo, 0, 0, PACK // 2)
-        deal(nc.scalar.copy, w1_lo, 0, PACK // 2, PACK)
-        deal(nc.vector.tensor_copy, w1_hi, M_HALF, 0, PACK // 2)
-        deal(nc.vector.tensor_copy, w1_hi, M_HALF, PACK // 2, PACK)
+        deal(nc.vector.tensor_copy, w1_early, 0, *tile_pairs[0])
+        deal(nc.scalar.copy, w1_early, 0, *tile_pairs[1])
+        for t0, t1 in tile_pairs:
+            deal(nc.vector.tensor_copy, w1_late, M_HALF, t0, t1)
 
-        lead_codes = keep.tile([P, HALF + V], U32, name="lead_codes", align_bytes=64)
-        lead_scales = keep.tile([P, V], U8, name="lead_scales", align_bytes=64)
-        x_codes = [lead_codes[:, HALF:], keep.tile([P, V], U32, name="x_codes1", align_bytes=64)[:]]
-        first_scales = lead_scales[:, HALF:]
+        lead_codes = keep.tile([P, WARM + V], U32, name="lead_codes", align_bytes=64)
+        lead_scales = keep.tile([P, WARM + EARLY], U8, name="lead_scales", align_bytes=64)
+        x_codes = [lead_codes[:, WARM:], keep.tile([P, V], U32, name="x_codes1", align_bytes=64)[:]]
+        early_scales = lead_scales[:, WARM:]
         late_scales = keep.tile([P, 2, V], U8, name="late_scales", tag="late", align_bytes=64)
         w1_codes = keep.tile([P, H], U32, name="w1_codes", align_bytes=64)
         w1_scales = keep.tile([P, H], U8, name="w1_scales", align_bytes=64)
 
         def x_scales(s, c0, c1):
-            if s == 0 and c1 <= NCH // 2:
-                return first_scales[:, c0 * CH : c1 * CH]
+            if s == 0 and c1 <= EARLY_CHUNKS:
+                return early_scales[:, c0 * CH : c1 * CH]
             return late_scales[:, s, c0 * CH : c1 * CH]
 
         def quantise_x(s, c0, c1):
@@ -102,36 +111,39 @@ def tile_picked_siam_abs_e_kernel(tc, xT, w1, w2_words, w2_scales, offs, out):
             nc.vector.quantize_mx(out=x_codes[s][:, cols].bitcast(FP8X4), scales=x_scales(s, c0, c1),
                                   in_=sides[s][:, cols, :].rearrange("p v j -> p (v j)"))
 
-        quantise_x(0, 0, 2)
-        nc.vector.quantize_mx(out=lead_codes[:, :HALF].bitcast(FP8X4), scales=lead_scales[:, :HALF], in_=last_bf[:, : PACK * HALF])
+        nc.vector.quantize_mx(out=lead_codes[:, :WARM].bitcast(FP8X4), scales=lead_scales[:, :WARM],
+                              in_=last_bf[:, LAST_PIECE - PACK * WARM : LAST_PIECE])
+        quantise_x(0, 0, EARLY_CHUNKS)
         idle = psum.tile([P, PACK, CH], F32, name="bank")
-        for width in (HALF, HALF, HALF, V):
+        for width in (WARM, WARM, WARM, WARM + EARLY):
             nc.tensor.matmul_mx(out=idle[:].rearrange("p t v -> p (t v)")[:, 0:width],
-                                lhsT=lead_codes[:, 0:P].bitcast(FP8X4), lhsT_scale=w2_plane[:, 0:P],
-                                rhs=lead_codes[:, 0:width].bitcast(FP8X4), rhs_scale=lead_scales[:, 0:width], start=True, stop=True)
-        for q in range(1, 4):
-            load_scales(q)
-        for t0, t1 in [[0, 2], [2, 4]]:
+                                lhsT=lead_codes[:, 0:P].bitcast(FP8X4), lhsT_scale=lead_scales[:, 0:P],
+                                rhs=lead_codes[:, 0:width].bitcast(FP8X4), rhs_scale=lead_scales[:, 0:width],
+                                start=True, stop=True)
+        for t0, t1 in tile_pairs:
             nc.vector.quantize_mx(out=w1_codes[:, t0 * P : t1 * P].bitcast(FP8X4), scales=w1_scales[:, t0 * P : t1 * P],
                                   in_=w1_bf[:, t0:t1, :, :].rearrange("p t m j -> p (t m j)"))
-        quantise_x(0, 2, 4)
-        quantise_x(1, 0, 2)
-        quantise_x(1, 2, 4)
+        quantise_x(0, EARLY_CHUNKS, NCH)
+        quantise_x(1, 0, NCH // 2)
+        quantise_x(1, NCH // 2, NCH)
 
-        def layer(s, c):
+        def first_product(s, c):
             bank = psum.tile([P, PACK, CH], F32, name="bank")
             for t in range(PACK):
-                m = slice(t * P, (t + 1) * P)
-                nc.tensor.matmul_mx(out=bank[:, t, :], lhsT=w1_codes[:, m].bitcast(FP8X4), lhsT_scale=w1_scales[:, m],
+                cols = slice(t * P, (t + 1) * P)
+                nc.tensor.matmul_mx(out=bank[:, t, :], lhsT=w1_codes[:, cols].bitcast(FP8X4), lhsT_scale=w1_scales[:, cols],
                                     rhs=x_codes[s][:, c * CH : (c + 1) * CH].bitcast(FP8X4),
                                     rhs_scale=x_scales(s, c, c + 1), start=True, stop=True)
             return bank
 
         banks = {}
-        for s, c in [[0, 0], [0, 1], [0, 2], [1, 0], [0, 3], [1, 1], [1, 2], [1, 3]]:
-            banks[s, c] = layer(s, c)
-        out_rows = out.rearrange("(h p) v -> p h v", p=P)
-        h_a = [ring.tile([P, CH, PACK], F32, name="h_a") for c in range(NCH)]
+        for step in range(NCH + SIDE_LEAD):
+            for s, c in ((1, step - SIDE_LEAD), (0, step)):
+                if 0 <= c < NCH:
+                    banks[s, c] = first_product(s, c)
+
+        out_rows = out.rearrange("(half p) v -> p half v", p=P)
+        h_first = [ring.tile([P, CH, PACK], F32, name="h_first") for c in range(NCH)]
         diff = [ring.tile([P, CH, PACK], BF16, name="diff", align_bytes=64) for c in range(NCH)]
         z = [ring.tile([P, CH * PACK], BF16, name="z", align_bytes=64) for c in range(NCH)]
         z_codes = [ring.tile([P, CH], U32, name="z_codes", align_bytes=64) for c in range(NCH)]
@@ -139,58 +151,59 @@ def tile_picked_siam_abs_e_kernel(tc, xT, w1, w2_words, w2_scales, offs, out):
 
         def relu(c):
             sums = banks[0, c][:].rearrange("p t v -> p v t")
-            if c == 1:
-                nc.vector.tensor_scalar(h_a[c][:], sums, 0.0, None, ALU.max)
+            if c == VECTOR_RELU:
+                nc.vector.tensor_scalar(h_first[c][:], sums, 0.0, None, ALU.max)
             else:
-                nc.scalar.activation(h_a[c][:], sums, ACT.Relu)
+                nc.scalar.activation(h_first[c][:], sums, ACT.Relu)
 
-        def sub(c):
-            nc.vector.scalar_tensor_tensor(diff[c][:], banks[1, c][:].rearrange("p t v -> p v t"), 0.0, h_a[c][:], ALU.max, ALU.subtract)
+        def difference(c):
+            nc.vector.scalar_tensor_tensor(diff[c][:], banks[1, c][:].rearrange("p t v -> p v t"), 0.0, h_first[c][:],
+                                           ALU.max, ALU.subtract)
 
-        def flat(c):
+        def flat_diff(c):
             return diff[c][:].rearrange("p v t -> p (v t)")
 
-        def mag_scalar(c, a, b):
-            nc.scalar.activation(z[c][:, a:b], flat(c)[:, a:b], ACT.Abs)
+        def magnitude_on_scalar(c, width):
+            nc.scalar.activation(z[c][:, 0:width], flat_diff(c)[:, 0:width], ACT.Abs)
 
         def quantise_z(c):
             nc.vector.quantize_mx(out=z_codes[c][:].bitcast(FP8X4), scales=z_scales[c][:], in_=z[c][:])
 
-        def project(acc, c, h):
-            nc.tensor.matmul_mx(out=acc, lhsT=w2_codes[:, 2 * P * h : 2 * P * (h + 1)].bitcast(FP4X4),
-                                lhsT_scale=w2_plane[:, P * h : P * (h + 1)],
+        def second_product(acc, c, half):
+            nc.tensor.matmul_mx(out=acc, lhsT=w2_codes[:, 2 * P * half : 2 * P * (half + 1)].bitcast(FP4X4),
+                                lhsT_scale=w2_scale_rows[:, P * half : P * (half + 1)],
                                 rhs=z_codes[c][:].bitcast(FP8X4), rhs_scale=z_scales[c][:], start=True, stop=True)
 
         def finish(c, copy):
             acc = psum.tile([P, PACK, CH], F32, name="bank")
-            for h in range(N // P):
-                project(acc[:, h, :], c, h)
+            for half in range(N // P):
+                second_product(acc[:, half, :], c, half)
             res = ring.tile([P, N // P, CH], F32, name="res")
             copy(res[:], acc[:, 0 : N // P, :])
             nc.sync.dma_start(out_rows[:, :, c * CH : (c + 1) * CH], res[:])
 
-        def finish_split(c):
-            for h, (copy, queue) in enumerate(((nc.vector.tensor_copy, nc.sync), (nc.scalar.copy, nc.scalar))):
+        def finish_in_halves(c):
+            for half, (copy, queue) in enumerate(((nc.vector.tensor_copy, nc.sync), (nc.scalar.copy, nc.scalar))):
                 acc = psum.tile([P, PACK, CH], F32, name="bank")
-                project(acc[:, 0, :], c, h)
-                part = keep.tile([P, CH], F32, name=f"part{h}")
+                second_product(acc[:, 0, :], c, half)
+                part = keep.tile([P, CH], F32, name=f"part{half}")
                 copy(part[:], acc[:, 0, :])
-                queue.dma_start(out_rows[:, h, c * CH : (c + 1) * CH], part[:])
+                queue.dma_start(out_rows[:, half, c * CH : (c + 1) * CH], part[:])
 
+        last = NCH - 1
         for c in range(NCH):
             relu(c)
         for c in range(NCH):
-            sub(c)
-        last = NCH - 1
+            difference(c)
         for c in range(last):
-            mag_scalar(c, 0, CH * PACK)
-        mag_scalar(last, 0, MAG_SCALAR)
+            magnitude_on_scalar(c, CH * PACK)
+        magnitude_on_scalar(last, MAG_SCALAR)
         quantise_z(0)
-        rest = flat(last)[:, MAG_SCALAR:]
+        rest = flat_diff(last)[:, MAG_SCALAR:]
         nc.vector.scalar_tensor_tensor(z[last][:, MAG_SCALAR:], rest, -1.0, rest, ALU.mult, ALU.max)
         for c in range(1, NCH):
             quantise_z(c)
-        finish(0, nc.scalar.copy)
-        finish(1, nc.scalar.copy)
-        finish(2, nc.vector.tensor_copy)
-        finish_split(3)
+        for c in range(last - 1):
+            finish(c, nc.scalar.copy)
+        finish(last - 1, nc.vector.tensor_copy)
+        finish_in_halves(last)

@@ -28,11 +28,11 @@ M_HALF = P // 2
 
 LAST_PIECE = T - 256
 PIECES = [(0, 1024), (1024, 2048), (2048, 3072), (3072, LAST_PIECE), (LAST_PIECE, T)]
-VECTOR_CASTS = [(2048, 3072), (3072, 3584)]
-SCALAR_CASTS = [(0, 1024), (1024, 2048), (3584, LAST_PIECE), (LAST_PIECE, T)]
+VECTOR_CASTS = [(0, 1024), (1024, 2048), (2048, 3072), (3072, 3584)]
+SCALAR_CASTS = [(3584, LAST_PIECE), (LAST_PIECE, T)]
 EARLY_CHUNKS = 2
 EARLY = EARLY_CHUNKS * CH
-WARM = 256
+WARM_PASSES = 4
 SIDE_LEAD = 3
 VECTOR_RELU = 1
 MAG_SCALAR = 320
@@ -71,8 +71,10 @@ def tile_picked_siam_abs_e_kernel(tc, xT, w1, w2_words, w2_scales, offs, out):
         sides = [keep.tile([P, V, PACK], BF16, name=f"side{s}", align_bytes=64) for s in range(2)]
         lists = [offsets[:, s * (V // LIST_GROUP) : (s + 1) * (V // LIST_GROUP)] for s in range(2)]
         for j in range(PACK - 1):
-            for s in range(2):
-                nc.vector.tensor_copy(sides[s][:, :, j], planes[j][:].indirect(lists[s]))
+            nc.vector.tensor_copy(sides[0][:, :, j], planes[j][:].indirect(lists[0]))
+            run = ring.tile([P, V], BF16, name="run")
+            nc.scalar.activation(run[:], planes[j][:].indirect(lists[1]), ACT.Copy)
+            nc.scalar.copy(sides[1][:, :, j], run[:])
         last_bf = keep.tile([P, T], BF16, name="last_bf", align_bytes=64)
         for a, b in VECTOR_CASTS:
             nc.vector.tensor_copy(last_bf[:, a:b], last_plane[:, a:b])
@@ -93,10 +95,8 @@ def tile_picked_siam_abs_e_kernel(tc, xT, w1, w2_words, w2_scales, offs, out):
         for t0, t1 in tile_pairs:
             deal(nc.vector.tensor_copy, w1_late, M_HALF, t0, t1)
 
-        lead_codes = keep.tile([P, WARM + V], U32, name="lead_codes", align_bytes=64)
-        lead_scales = keep.tile([P, WARM + EARLY], U8, name="lead_scales", align_bytes=64)
-        x_codes = [lead_codes[:, WARM:], keep.tile([P, V], U32, name="x_codes1", align_bytes=64)[:]]
-        early_scales = lead_scales[:, WARM:]
+        x_codes = [keep.tile([P, V], U32, name=f"x_codes{s}", align_bytes=64) for s in range(2)]
+        early_scales = keep.tile([P, EARLY], U8, name="early_scales", align_bytes=64)
         late_scales = keep.tile([P, 2, V], U8, name="late_scales", tag="late", align_bytes=64)
         w1_codes = keep.tile([P, H], U32, name="w1_codes", align_bytes=64)
         w1_scales = keep.tile([P, H], U8, name="w1_scales", align_bytes=64)
@@ -111,14 +111,12 @@ def tile_picked_siam_abs_e_kernel(tc, xT, w1, w2_words, w2_scales, offs, out):
             nc.vector.quantize_mx(out=x_codes[s][:, cols].bitcast(FP8X4), scales=x_scales(s, c0, c1),
                                   in_=sides[s][:, cols, :].rearrange("p v j -> p (v j)"))
 
-        nc.vector.quantize_mx(out=lead_codes[:, :WARM].bitcast(FP8X4), scales=lead_scales[:, :WARM],
-                              in_=last_bf[:, LAST_PIECE - PACK * WARM : LAST_PIECE])
         quantise_x(0, 0, EARLY_CHUNKS)
         idle = psum.tile([P, PACK, CH], F32, name="bank")
-        for width in (WARM, WARM, WARM, WARM + EARLY):
-            nc.tensor.matmul_mx(out=idle[:].rearrange("p t v -> p (t v)")[:, 0:width],
-                                lhsT=lead_codes[:, 0:P].bitcast(FP8X4), lhsT_scale=lead_scales[:, 0:P],
-                                rhs=lead_codes[:, 0:width].bitcast(FP8X4), rhs_scale=lead_scales[:, 0:width],
+        for rep in range(WARM_PASSES):
+            nc.tensor.matmul_mx(out=idle[:].rearrange("p t v -> p (t v)")[:, 0:EARLY],
+                                lhsT=x_codes[0][:, 0:P].bitcast(FP8X4), lhsT_scale=early_scales[:, 0:P],
+                                rhs=x_codes[0][:, 0:EARLY].bitcast(FP8X4), rhs_scale=early_scales[:],
                                 start=True, stop=True)
         for t0, t1 in tile_pairs:
             nc.vector.quantize_mx(out=w1_codes[:, t0 * P : t1 * P].bitcast(FP8X4), scales=w1_scales[:, t0 * P : t1 * P],

@@ -32,7 +32,7 @@ VECTOR_CASTS = [(0, 1024), (1024, 2048), (2048, 3072), (3072, 3584)]
 SCALAR_CASTS = [(3584, LAST_PIECE), (LAST_PIECE, T)]
 EARLY_CHUNKS = 2
 EARLY = EARLY_CHUNKS * CH
-WARM_PASSES = 4
+WARM_PASSES, WARM_M, WARM_N = 4, 32, 512
 SIDE_LEAD = 3
 VECTOR_RELU = 1
 MAG_SCALAR = 320
@@ -53,28 +53,34 @@ def tile_picked_siam_abs_e_kernel(tc, xT, w1, w2_words, w2_scales, offs, out):
         nc.vector.memset(w2_scale_rows[:].bitcast(I32), 0)
         nc.sync.dma_start(planes[0][:], x_rows[:, 0, :])
         nc.sync.dma_start(offsets[:], offs)
+
+        def load_scale_rows(q, c0, c1):
+            nc.sync.dma_start(w2_scale_rows[QUADRANT * q : QUADRANT * q + SCALE_ROWS, c0:c1].bitcast(I32),
+                              w2_scales[0, SCALE_ROWS * q : SCALE_ROWS * (q + 1), c0:c1].bitcast(I32))
+
+        for q in range(1, P // QUADRANT):
+            load_scale_rows(q, 0, N)
         for j in range(1, PACK - 1):
             nc.sync.dma_start(planes[j][:], x_rows[:, j, :])
         for a, b in PIECES:
             nc.sync.dma_start(last_plane[:, a:b], x_rows[:, PACK - 1, a:b])
+        load_scale_rows(0, 0, P)
         w1_rows = w1.rearrange("(p j) c -> p j c", j=PACK)
         w1_early = keep.tile([P, PACK, H // 2], F32, name="w1_early")
         w1_late = keep.tile([P, PACK, H // 2], F32, name="w1_late", tag="late", align_bytes=64)
         w2_codes = keep.tile([P, 2 * N], U8, name="w2_codes", align_bytes=64)
         nc.sync.dma_start(w1_early[:], w1_rows[:, :, : H // 2])
+        load_scale_rows(0, P, N)
         nc.sync.dma_start(w1_late[:], w1_rows[:, :, H // 2 :])
         nc.sync.dma_start(w2_codes[:].bitcast(I32), w2_words[0].bitcast(I32))
-        for q in range(P // QUADRANT):
-            nc.sync.dma_start(w2_scale_rows[QUADRANT * q : QUADRANT * q + SCALE_ROWS, :].bitcast(I32),
-                              w2_scales[0, SCALE_ROWS * q : SCALE_ROWS * (q + 1), :].bitcast(I32))
 
         sides = [keep.tile([P, V, PACK], BF16, name=f"side{s}", align_bytes=64) for s in range(2)]
         lists = [offsets[:, s * (V // LIST_GROUP) : (s + 1) * (V // LIST_GROUP)] for s in range(2)]
+        runs = keep.tile([P, PACK - 1, V], BF16, name="runs", align_bytes=64)
         for j in range(PACK - 1):
             nc.vector.tensor_copy(sides[0][:, :, j], planes[j][:].indirect(lists[0]))
-            run = ring.tile([P, V], BF16, name="run")
-            nc.scalar.activation(run[:], planes[j][:].indirect(lists[1]), ACT.Copy)
-            nc.scalar.copy(sides[1][:, :, j], run[:])
+            nc.scalar.activation(runs[:, j, :], planes[j][:].indirect(lists[1]), ACT.Copy)
+            nc.scalar.copy(sides[1][:, :, j], runs[:, j, :])
         last_bf = keep.tile([P, T], BF16, name="last_bf", align_bytes=64)
         for a, b in VECTOR_CASTS:
             nc.vector.tensor_copy(last_bf[:, a:b], last_plane[:, a:b])
@@ -112,12 +118,18 @@ def tile_picked_siam_abs_e_kernel(tc, xT, w1, w2_words, w2_scales, offs, out):
                                   in_=sides[s][:, cols, :].rearrange("p v j -> p (v j)"))
 
         quantise_x(0, 0, EARLY_CHUNKS)
-        idle = psum.tile([P, PACK, CH], F32, name="bank")
+        warm_codes = keep.tile([P, WARM_N], U32, name="warm_codes", align_bytes=64)
+        warm_scales = keep.tile([P, WARM_N], U8, name="warm_scales", align_bytes=64)
+        for h in range(2):
+            cols = slice(h * WARM_N // 2, (h + 1) * WARM_N // 2)
+            nc.vector.quantize_mx(out=warm_codes[:, cols].bitcast(FP8X4), scales=warm_scales[:, cols],
+                                  in_=runs[:, 0:2, :].rearrange("p j v -> p (j v)"))
+        idle = psum.tile([P, WARM_N], F32, name="bank")
         for rep in range(WARM_PASSES):
-            nc.tensor.matmul_mx(out=idle[:].rearrange("p t v -> p (t v)")[:, 0:EARLY],
-                                lhsT=x_codes[0][:, 0:P].bitcast(FP8X4), lhsT_scale=early_scales[:, 0:P],
-                                rhs=x_codes[0][:, 0:EARLY].bitcast(FP8X4), rhs_scale=early_scales[:],
-                                start=True, stop=True)
+            first = P * (2 * rep // WARM_PASSES)
+            nc.tensor.matmul_mx(out=idle[0:WARM_M, :], lhsT=warm_codes[:, 0:WARM_M].bitcast(FP8X4),
+                                lhsT_scale=w2_scale_rows[:, first : first + WARM_M], rhs=warm_codes[:].bitcast(FP8X4),
+                                rhs_scale=warm_scales[:], start=True, stop=True)
         for t0, t1 in tile_pairs:
             nc.vector.quantize_mx(out=w1_codes[:, t0 * P : t1 * P].bitcast(FP8X4), scales=w1_scales[:, t0 * P : t1 * P],
                                   in_=w1_bf[:, t0:t1, :, :].rearrange("p t m j -> p (t m j)"))

@@ -64,14 +64,14 @@ def tile_picked_siam_abs_e_kernel(tc, xT, w1, w2_words, w2_scales, offs, out):
             nc.sync.dma_start(planes[j][:], x_rows[:, j, :])
         for a, b in PIECES:
             nc.sync.dma_start(last_plane[:, a:b], x_rows[:, PACK - 1, a:b])
-        load_scale_rows(0, 0, P)
         w1_rows = w1.rearrange("(p j) c -> p j c", j=PACK)
         w1_early = keep.tile([P, PACK, H // 2], F32, name="w1_early")
         w1_late = keep.tile([P, PACK, H // 2], F32, name="w1_late", tag="late", align_bytes=64)
         w2_codes = keep.tile([P, 2 * N], U8, name="w2_codes", align_bytes=64)
         nc.sync.dma_start(w1_early[:], w1_rows[:, :, : H // 2])
-        load_scale_rows(0, P, N)
+        load_scale_rows(0, 0, P)
         nc.sync.dma_start(w1_late[:], w1_rows[:, :, H // 2 :])
+        load_scale_rows(0, P, N)
         nc.sync.dma_start(w2_codes[:].bitcast(I32), w2_words[0].bitcast(I32))
 
         sides = [keep.tile([P, V, PACK], BF16, name=f"side{s}", align_bytes=64) for s in range(2)]

@@ -32,7 +32,8 @@ VECTOR_CASTS = [(0, 1024), (1024, 2048), (2048, 3072), (3072, 3584)]
 SCALAR_CASTS = [(3584, LAST_PIECE), (LAST_PIECE, T)]
 EARLY_CHUNKS = 2
 EARLY = EARLY_CHUNKS * CH
-WARM_PASSES, WARM_M, WARM_N = 4, 32, 512
+WARM_M, WARM_N = 32, 512
+WARM_STARTS = [(0, 64), (64, 128), (128, N)]
 SIDE_LEAD = 3
 VECTOR_RELU = 1
 MAG_SCALAR = 320
@@ -64,14 +65,15 @@ def tile_picked_siam_abs_e_kernel(tc, xT, w1, w2_words, w2_scales, offs, out):
             nc.sync.dma_start(planes[j][:], x_rows[:, j, :])
         for a, b in PIECES:
             nc.sync.dma_start(last_plane[:, a:b], x_rows[:, PACK - 1, a:b])
+        load_scale_rows(0, *WARM_STARTS[0])
         w1_rows = w1.rearrange("(p j) c -> p j c", j=PACK)
         w1_early = keep.tile([P, PACK, H // 2], F32, name="w1_early")
         w1_late = keep.tile([P, PACK, H // 2], F32, name="w1_late", tag="late", align_bytes=64)
         w2_codes = keep.tile([P, 2 * N], U8, name="w2_codes", align_bytes=64)
         nc.sync.dma_start(w1_early[:], w1_rows[:, :, : H // 2])
-        load_scale_rows(0, 0, P)
+        load_scale_rows(0, *WARM_STARTS[1])
         nc.sync.dma_start(w1_late[:], w1_rows[:, :, H // 2 :])
-        load_scale_rows(0, P, N)
+        load_scale_rows(0, *WARM_STARTS[2])
         nc.sync.dma_start(w2_codes[:].bitcast(I32), w2_words[0].bitcast(I32))
 
         sides = [keep.tile([P, V, PACK], BF16, name=f"side{s}", align_bytes=64) for s in range(2)]
@@ -125,8 +127,8 @@ def tile_picked_siam_abs_e_kernel(tc, xT, w1, w2_words, w2_scales, offs, out):
             nc.vector.quantize_mx(out=warm_codes[:, cols].bitcast(FP8X4), scales=warm_scales[:, cols],
                                   in_=runs[:, 0:2, :].rearrange("p j v -> p (j v)"))
         idle = psum.tile([P, WARM_N], F32, name="bank")
-        for rep in range(WARM_PASSES):
-            first = P * (2 * rep // WARM_PASSES)
+        for start in (0, 1, 1, 2):
+            first = WARM_STARTS[start][0]
             nc.tensor.matmul_mx(out=idle[0:WARM_M, :], lhsT=warm_codes[:, 0:WARM_M].bitcast(FP8X4),
                                 lhsT_scale=w2_scale_rows[:, first : first + WARM_M], rhs=warm_codes[:].bitcast(FP8X4),
                                 rhs_scale=warm_scales[:], start=True, stop=True)

@@ -32,8 +32,10 @@ VECTOR_CASTS = [(0, 1024), (1024, 2048), (2048, 3072), (3072, 3584)]
 SCALAR_CASTS = [(3584, LAST_PIECE), (LAST_PIECE, T)]
 EARLY_CHUNKS = 2
 EARLY = EARLY_CHUNKS * CH
+EARLY_AT = 192
+LATE_RUN = 1
 WARM_M, WARM_N = 32, 512
-WARM_STARTS = [(0, 64), (64, 128), (128, N)]
+WARM_STARTS = [(0, 64), (128, N), (64, 128)]
 SIDE_LEAD = 3
 VECTOR_RELU = 1
 MAG_SCALAR = 320
@@ -50,8 +52,8 @@ def tile_picked_siam_abs_e_kernel(tc, xT, w1, w2_words, w2_scales, offs, out):
         x_rows = xT.rearrange("(p j) w -> p j w", j=PACK)
         planes = [keep.tile([P, T], F32, name=f"plane{j}") for j in range(PACK)]
         last_plane = planes[PACK - 1]
-        w2_scale_rows = keep.tile([P, N], U8, name="w2_scale_rows", align_bytes=64)
-        nc.vector.memset(w2_scale_rows[:].bitcast(I32), 0)
+        w2_scale_rows = keep.tile([P, EARLY_AT + EARLY], U8, name="w2_scale_rows", align_bytes=64)
+        nc.vector.memset(w2_scale_rows[:, 0:N].bitcast(I32), 0)
         nc.sync.dma_start(planes[0][:], x_rows[:, 0, :])
         nc.sync.dma_start(offsets[:], offs)
 
@@ -59,21 +61,22 @@ def tile_picked_siam_abs_e_kernel(tc, xT, w1, w2_words, w2_scales, offs, out):
             nc.sync.dma_start(w2_scale_rows[QUADRANT * q : QUADRANT * q + SCALE_ROWS, c0:c1].bitcast(I32),
                               w2_scales[0, SCALE_ROWS * q : SCALE_ROWS * (q + 1), c0:c1].bitcast(I32))
 
-        for q in range(1, P // QUADRANT):
-            load_scale_rows(q, 0, N)
+        for q in range(P // QUADRANT):
+            if q != LATE_RUN:
+                load_scale_rows(q, 0, N)
         for j in range(1, PACK - 1):
             nc.sync.dma_start(planes[j][:], x_rows[:, j, :])
         for a, b in PIECES:
             nc.sync.dma_start(last_plane[:, a:b], x_rows[:, PACK - 1, a:b])
-        load_scale_rows(0, *WARM_STARTS[0])
+        load_scale_rows(LATE_RUN, *WARM_STARTS[0])
         w1_rows = w1.rearrange("(p j) c -> p j c", j=PACK)
         w1_early = keep.tile([P, PACK, H // 2], F32, name="w1_early")
         w1_late = keep.tile([P, PACK, H // 2], F32, name="w1_late", tag="late", align_bytes=64)
         w2_codes = keep.tile([P, 2 * N], U8, name="w2_codes", align_bytes=64)
         nc.sync.dma_start(w1_early[:], w1_rows[:, :, : H // 2])
-        load_scale_rows(0, *WARM_STARTS[1])
+        load_scale_rows(LATE_RUN, *WARM_STARTS[1])
         nc.sync.dma_start(w1_late[:], w1_rows[:, :, H // 2 :])
-        load_scale_rows(0, *WARM_STARTS[2])
+        load_scale_rows(LATE_RUN, *WARM_STARTS[2])
         nc.sync.dma_start(w2_codes[:].bitcast(I32), w2_words[0].bitcast(I32))
 
         sides = [keep.tile([P, V, PACK], BF16, name=f"side{s}", align_bytes=64) for s in range(2)]
@@ -104,14 +107,13 @@ def tile_picked_siam_abs_e_kernel(tc, xT, w1, w2_words, w2_scales, offs, out):
             deal(nc.vector.tensor_copy, w1_late, M_HALF, t0, t1)
 
         x_codes = [keep.tile([P, V], U32, name=f"x_codes{s}", align_bytes=64) for s in range(2)]
-        early_scales = keep.tile([P, EARLY], U8, name="early_scales", align_bytes=64)
         late_scales = keep.tile([P, 2, V], U8, name="late_scales", tag="late", align_bytes=64)
         w1_codes = keep.tile([P, H], U32, name="w1_codes", align_bytes=64)
         w1_scales = keep.tile([P, H], U8, name="w1_scales", align_bytes=64)
 
         def x_scales(s, c0, c1):
             if s == 0 and c1 <= EARLY_CHUNKS:
-                return early_scales[:, c0 * CH : c1 * CH]
+                return w2_scale_rows[SCALE_ROWS:P, EARLY_AT + c0 * CH : EARLY_AT + c1 * CH]
             return late_scales[:, s, c0 * CH : c1 * CH]
 
         def quantise_x(s, c0, c1):

@@ -27,9 +27,9 @@ NCH = V // CH
 M_HALF = P // 2
 
 LAST_PIECE = T - 256
-PIECES = [(0, 1024), (1024, 2048), (2048, 3072), (3072, LAST_PIECE), (LAST_PIECE, T)]
-VECTOR_CASTS = [(0, 1024), (1024, 2048), (2048, 3072), (3072, 3584)]
-SCALAR_CASTS = [(3584, LAST_PIECE), (LAST_PIECE, T)]
+PIECES = [(0, 2048), (2048, 3072), (3072, 3584), (3584, LAST_PIECE), (LAST_PIECE, T)]
+VECTOR_CASTS = PIECES[:-1]
+SCALAR_CASTS = PIECES[-1:]
 EARLY_CHUNKS = 2
 EARLY = EARLY_CHUNKS * CH
 EARLY_AT = 192

@@ -197,12 +197,12 @@ def tile_picked_siam_abs_e_kernel(tc, xT, w1, w2_words, w2_scales, offs, out):
             nc.sync.dma_start(out_rows[:, :, c * CH : (c + 1) * CH], res[:])
 
         def finish_in_halves(c):
-            for half, (copy, queue) in enumerate(((nc.vector.tensor_copy, nc.sync), (nc.scalar.copy, nc.scalar))):
+            for half, copy in enumerate((nc.scalar.copy, nc.vector.tensor_copy)):
                 acc = psum.tile([P, PACK, CH], F32, name="bank")
                 second_product(acc[:, 0, :], c, half)
-                part = keep.tile([P, CH], F32, name=f"part{half}")
+                part = ring.tile([P, CH], F32, name="part")
                 copy(part[:], acc[:, 0, :])
-                queue.dma_start(out_rows[:, half, c * CH : (c + 1) * CH], part[:])
+                nc.sync.dma_start(out_rows[:, half, c * CH : (c + 1) * CH], part[:])
 
         last = NCH - 1
         for c in range(NCH):
@@ -219,5 +219,5 @@ def tile_picked_siam_abs_e_kernel(tc, xT, w1, w2_words, w2_scales, offs, out):
             quantise_z(c)
         for c in range(last - 1):
             finish(c, nc.scalar.copy)
-        finish(last - 1, nc.vector.tensor_copy)
+        finish_in_halves(last - 1)
         finish_in_halves(last)

@@ -22,6 +22,7 @@ LIST_GROUP = 16
 QUADRANT = 32
 SCALE_ROWS = 4
 BANKS = 8
+UNIT_SCALES = 0x7F7F7F7F
 CH = 128
 NCH = V // CH
 M_HALF = P // 2
@@ -53,7 +54,7 @@ def tile_picked_siam_abs_e_kernel(tc, xT, w1, w2_words, w2_scales, offs, out):
         planes = [keep.tile([P, T], F32, name=f"plane{j}") for j in range(PACK)]
         last_plane = planes[PACK - 1]
         w2_scale_rows = keep.tile([P, EARLY_AT + EARLY], U8, name="w2_scale_rows", align_bytes=64)
-        nc.vector.memset(w2_scale_rows[:, 0:N].bitcast(I32), 0)
+        nc.vector.memset(w2_scale_rows[:, 0:N].bitcast(I32), UNIT_SCALES)
         nc.sync.dma_start(planes[0][:], x_rows[:, 0, :])
         nc.sync.dma_start(offsets[:], offs)
 
@@ -61,9 +62,6 @@ def tile_picked_siam_abs_e_kernel(tc, xT, w1, w2_words, w2_scales, offs, out):
             nc.sync.dma_start(w2_scale_rows[QUADRANT * q : QUADRANT * q + SCALE_ROWS, c0:c1].bitcast(I32),
                               w2_scales[0, SCALE_ROWS * q : SCALE_ROWS * (q + 1), c0:c1].bitcast(I32))
 
-        for q in range(P // QUADRANT):
-            if q != LATE_RUN:
-                load_scale_rows(q, 0, N)
         for j in range(1, PACK - 1):
             nc.sync.dma_start(planes[j][:], x_rows[:, j, :])
         for a, b in PIECES:
@@ -155,6 +153,10 @@ def tile_picked_siam_abs_e_kernel(tc, xT, w1, w2_words, w2_scales, offs, out):
             for s, c in ((1, step - SIDE_LEAD), (0, step)):
                 if 0 <= c < NCH:
                     banks[s, c] = first_product(s, c)
+
+        for q in range(P // QUADRANT):
+            if q != LATE_RUN:
+                load_scale_rows(q, 0, N)
 
         out_rows = out.rearrange("(half p) v -> p half v", p=P)
         h_first = [ring.tile([P, CH, PACK], F32, name="h_first") for c in range(NCH)]

@@ -22,6 +22,7 @@ LIST_GROUP = 16
 QUADRANT = 32
 SCALE_ROWS = 4
 BANKS = 8
+DMA_ALIGN = 256
 UNIT_SCALES = 0x7F7F7F7F
 CH = 128
 NCH = V // CH
@@ -51,7 +52,7 @@ def tile_picked_siam_abs_e_kernel(tc, xT, w1, w2_words, w2_scales, offs, out):
 
         offsets = keep.tile([P, S // LIST_GROUP], U16, name="offsets")
         x_rows = xT.rearrange("(p j) w -> p j w", j=PACK)
-        planes = [keep.tile([P, T], F32, name=f"plane{j}") for j in range(PACK)]
+        planes = [keep.tile([P, T], F32, name=f"plane{j}", align_bytes=DMA_ALIGN) for j in range(PACK)]
         last_plane = planes[PACK - 1]
         w2_scale_rows = keep.tile([P, EARLY_AT + EARLY], U8, name="w2_scale_rows", align_bytes=64)
         nc.vector.memset(w2_scale_rows[:, 0:N].bitcast(I32), UNIT_SCALES)
@@ -68,8 +69,8 @@ def tile_picked_siam_abs_e_kernel(tc, xT, w1, w2_words, w2_scales, offs, out):
             nc.sync.dma_start(last_plane[:, a:b], x_rows[:, PACK - 1, a:b])
         load_scale_rows(LATE_RUN, *WARM_STARTS[0])
         w1_rows = w1.rearrange("(p j) c -> p j c", j=PACK)
-        w1_early = keep.tile([P, PACK, H // 2], F32, name="w1_early")
-        w1_late = keep.tile([P, PACK, H // 2], F32, name="w1_late", tag="late", align_bytes=64)
+        w1_early = keep.tile([P, PACK, H // 2], F32, name="w1_early", align_bytes=DMA_ALIGN)
+        w1_late = keep.tile([P, PACK, H // 2], F32, name="w1_late", tag="late", align_bytes=DMA_ALIGN)
         w2_codes = keep.tile([P, 2 * N], U8, name="w2_codes", align_bytes=64)
         nc.sync.dma_start(w1_early[:], w1_rows[:, :, : H // 2])
         load_scale_rows(LATE_RUN, *WARM_STARTS[1])
@@ -105,7 +106,7 @@ def tile_picked_siam_abs_e_kernel(tc, xT, w1, w2_words, w2_scales, offs, out):
             deal(nc.vector.tensor_copy, w1_late, M_HALF, t0, t1)
 
         x_codes = [keep.tile([P, V], U32, name=f"x_codes{s}", align_bytes=64) for s in range(2)]
-        late_scales = keep.tile([P, 2, V], U8, name="late_scales", tag="late", align_bytes=64)
+        late_scales = keep.tile([P, 2, V], U8, name="late_scales", tag="late", align_bytes=DMA_ALIGN)
         w1_codes = keep.tile([P, H], U32, name="w1_codes", align_bytes=64)
         w1_scales = keep.tile([P, H], U8, name="w1_scales", align_bytes=64)
 
@@ -194,7 +195,7 @@ def tile_picked_siam_abs_e_kernel(tc, xT, w1, w2_words, w2_scales, offs, out):
             acc = psum.tile([P, PACK, CH], F32, name="bank")
             for half in range(N // P):
                 second_product(acc[:, half, :], c, half)
-            res = ring.tile([P, N // P, CH], F32, name="res")
+            res = ring.tile([P, N // P, CH], F32, name="res", align_bytes=DMA_ALIGN)
             copy(res[:], acc[:, 0 : N // P, :])
             nc.sync.dma_start(out_rows[:, :, c * CH : (c + 1) * CH], res[:])
 
@@ -202,7 +203,7 @@ def tile_picked_siam_abs_e_kernel(tc, xT, w1, w2_words, w2_scales, offs, out):
             for half, copy in enumerate((nc.scalar.copy, nc.vector.tensor_copy)):
                 acc = psum.tile([P, PACK, CH], F32, name="bank")
                 second_product(acc[:, 0, :], c, half)
-                part = ring.tile([P, CH], F32, name="part")
+                part = ring.tile([P, CH], F32, name="part", align_bytes=DMA_ALIGN)
                 copy(part[:], acc[:, 0, :])
                 nc.sync.dma_start(out_rows[:, half, c * CH : (c + 1) * CH], part[:])
 

@@ -210,17 +210,19 @@ def tile_picked_siam_abs_e_kernel(tc, xT, w1, w2_words, w2_scales, offs, out):
         last = NCH - 1
         for c in range(NCH):
             relu(c)
-        for c in range(NCH):
+        for c in range(last):
             difference(c)
         for c in range(last):
             magnitude_on_scalar(c, CH * PACK)
-        magnitude_on_scalar(last, MAG_SCALAR)
         quantise_z(0)
+        difference(last)
+        finish(0, nc.scalar.copy)
+        quantise_z(1)
+        magnitude_on_scalar(last, MAG_SCALAR)
         rest = flat_diff(last)[:, MAG_SCALAR:]
         nc.vector.scalar_tensor_tensor(z[last][:, MAG_SCALAR:], rest, -1.0, rest, ALU.mult, ALU.max)
-        for c in range(1, NCH):
+        finish(1, nc.scalar.copy)
+        for c in range(2, NCH):
             quantise_z(c)
-        for c in range(last - 1):
-            finish(c, nc.scalar.copy)
         finish_in_halves(last - 1)
         finish_in_halves(last)

from contextlib import ExitStack

import concourse.mybir as mybir

K, T, S, V, H, N = 512, 4096, 1024, 512, 512, 256
FLOPS = 2 * K * H * S + 2 * H * N * V

F32 = mybir.dt.float32
BF16 = mybir.dt.bfloat16
I32 = mybir.dt.int32
U32 = mybir.dt.uint32
U16 = mybir.dt.uint16
U8 = mybir.dt.uint8
FP8X4 = mybir.dt.float8_e4m3fn_x4
FP4X4 = mybir.dt.float4_e2m1fn_x4
ACT = mybir.ActivationFunctionType
ALU = mybir.AluOpType

P = 128
PACK = 4
LIST_GROUP = 16
QUADRANT = 32
SCALE_ROWS = 4
BANKS = 8
DMA_ALIGN = 256
UNIT_SCALES = 0x7F7F7F7F
CH = 128
NCH = V // CH
M_HALF = P // 2

LAST_PIECE = T - 256
PIECES = [(0, 2048), (2048, 3072), (3072, 3584), (3584, LAST_PIECE), (LAST_PIECE, T)]
VECTOR_CASTS = PIECES[:-1]
SCALAR_CASTS = PIECES[-1:]
EARLY_CHUNKS = 2
EARLY = EARLY_CHUNKS * CH
EARLY_AT = 192
LATE_RUN = 1
WARM_M, WARM_N = 32, 512
WARM_STARTS = [(0, 64), (128, N), (64, 128)]
SIDE_LEAD = 3
VECTOR_RELU = 1
MAG_SCALAR = 320


def tile_picked_siam_abs_e_kernel(tc, xT, w1, w2_words, w2_scales, offs, out):
    nc = tc.nc
    with ExitStack() as ctx:
        keep = ctx.enter_context(tc.tile_pool(name="keep", bufs=1))
        ring = ctx.enter_context(tc.tile_pool(name="ring", bufs=NCH))
        psum = ctx.enter_context(tc.psum_pool(name="psum", bufs=BANKS))

        offsets = keep.tile([P, S // LIST_GROUP], U16, name="offsets")
        x_rows = xT.rearrange("(p j) w -> p j w", j=PACK)
        planes = [keep.tile([P, T], F32, name=f"plane{j}", align_bytes=DMA_ALIGN) for j in range(PACK)]
        last_plane = planes[PACK - 1]
        w2_scale_rows = keep.tile([P, EARLY_AT + EARLY], U8, name="w2_scale_rows", align_bytes=64)
        nc.vector.memset(w2_scale_rows[:, 0:N].bitcast(I32), UNIT_SCALES)
        nc.sync.dma_start(planes[0][:], x_rows[:, 0, :])
        nc.sync.dma_start(offsets[:], offs)

        def load_scale_rows(q, c0, c1):
            nc.sync.dma_start(w2_scale_rows[QUADRANT * q : QUADRANT * q + SCALE_ROWS, c0:c1].bitcast(I32),
                              w2_scales[0, SCALE_ROWS * q : SCALE_ROWS * (q + 1), c0:c1].bitcast(I32))

        for j in range(1, PACK - 1):
            nc.sync.dma_start(planes[j][:], x_rows[:, j, :])
        for a, b in PIECES:
            nc.sync.dma_start(last_plane[:, a:b], x_rows[:, PACK - 1, a:b])
        load_scale_rows(LATE_RUN, *WARM_STARTS[0])
        w1_rows = w1.rearrange("(p j) c -> p j c", j=PACK)
        w1_early = keep.tile([P, PACK, H // 2], F32, name="w1_early", align_bytes=DMA_ALIGN)
        w1_late = keep.tile([P, PACK, H // 2], F32, name="w1_late", tag="late", align_bytes=DMA_ALIGN)
        w2_codes = keep.tile([P, 2 * N], U8, name="w2_codes", align_bytes=64)
        nc.sync.dma_start(w1_early[:], w1_rows[:, :, : H // 2])
        load_scale_rows(LATE_RUN, *WARM_STARTS[1])
        nc.sync.dma_start(w1_late[:], w1_rows[:, :, H // 2 :])
        load_scale_rows(LATE_RUN, *WARM_STARTS[2])
        nc.sync.dma_start(w2_codes[:].bitcast(I32), w2_words[0].bitcast(I32))

        sides = [keep.tile([P, V, PACK], BF16, name=f"side{s}", align_bytes=64) for s in range(2)]
        lists = [offsets[:, s * (V // LIST_GROUP) : (s + 1) * (V // LIST_GROUP)] for s in range(2)]
        runs = keep.tile([P, PACK - 1, V], BF16, name="runs", align_bytes=64)
        for j in range(PACK - 1):
            nc.vector.tensor_copy(sides[0][:, :, j], planes[j][:].indirect(lists[0]))
            nc.scalar.activation(runs[:, j, :], planes[j][:].indirect(lists[1]), ACT.Copy)
            nc.scalar.copy(sides[1][:, :, j], runs[:, j, :])
        last_bf = keep.tile([P, T], BF16, name="last_bf", align_bytes=64)
        for a, b in VECTOR_CASTS:
            nc.vector.tensor_copy(last_bf[:, a:b], last_plane[:, a:b])
        for a, b in SCALAR_CASTS:
            nc.scalar.copy(last_bf[:, a:b], last_plane[:, a:b])
        nc.vector.tensor_copy(sides[0][:, :, PACK - 1], last_plane[:].indirect(lists[0]))
        nc.scalar.activation(sides[1][:, :, PACK - 1], last_bf[:].indirect(lists[1]), ACT.Copy)

        w1_bf = keep.tile([P, PACK, P, PACK], BF16, name="w1_bf", align_bytes=64)
        tile_pairs = [(0, PACK // 2), (PACK // 2, PACK)]

        def deal(copy, raw, m_base, t0, t1):
            copy(w1_bf[:, t0:t1, m_base : m_base + M_HALF, :].rearrange("p t m j -> p m j t"),
                 raw[:].rearrange("p j (m t) -> p m j t", t=PACK)[:, :, :, t0:t1])

        deal(nc.vector.tensor_copy, w1_early, 0, *tile_pairs[0])
        deal(nc.scalar.copy, w1_early, 0, *tile_pairs[1])
        for t0, t1 in tile_pairs:
            deal(nc.vector.tensor_copy, w1_late, M_HALF, t0, t1)

        x_codes = [keep.tile([P, V], U32, name=f"x_codes{s}", align_bytes=64) for s in range(2)]
        late_scales = keep.tile([P, 2, V], U8, name="late_scales", tag="late", align_bytes=DMA_ALIGN)
        w1_codes = keep.tile([P, H], U32, name="w1_codes", align_bytes=64)
        w1_scales = keep.tile([P, H], U8, name="w1_scales", align_bytes=64)

        def x_scales(s, c0, c1):
            if s == 0 and c1 <= EARLY_CHUNKS:
                return w2_scale_rows[SCALE_ROWS:P, EARLY_AT + c0 * CH : EARLY_AT + c1 * CH]
            return late_scales[:, s, c0 * CH : c1 * CH]

        def quantise_x(s, c0, c1):
            cols = slice(c0 * CH, c1 * CH)
            nc.vector.quantize_mx(out=x_codes[s][:, cols].bitcast(FP8X4), scales=x_scales(s, c0, c1),
                                  in_=sides[s][:, cols, :].rearrange("p v j -> p (v j)"))

        quantise_x(0, 0, EARLY_CHUNKS)
        warm_codes = keep.tile([P, WARM_N], U32, name="warm_codes", align_bytes=64)
        warm_scales = keep.tile([P, WARM_N], U8, name="warm_scales", align_bytes=64)
        for h in range(2):
            cols = slice(h * WARM_N // 2, (h + 1) * WARM_N // 2)
            nc.vector.quantize_mx(out=warm_codes[:, cols].bitcast(FP8X4), scales=warm_scales[:, cols],
                                  in_=runs[:, 0:2, :].rearrange("p j v -> p (j v)"))
        idle = psum.tile([P, WARM_N], F32, name="bank")
        for start in (0, 1, 1, 2):
            first = WARM_STARTS[start][0]
            nc.tensor.matmul_mx(out=idle[0:WARM_M, :], lhsT=warm_codes[:, 0:WARM_M].bitcast(FP8X4),
                                lhsT_scale=w2_scale_rows[:, first : first + WARM_M], rhs=warm_codes[:].bitcast(FP8X4),
                                rhs_scale=warm_scales[:], start=True, stop=True)
        for t0, t1 in tile_pairs:
            nc.vector.quantize_mx(out=w1_codes[:, t0 * P : t1 * P].bitcast(FP8X4), scales=w1_scales[:, t0 * P : t1 * P],
                                  in_=w1_bf[:, t0:t1, :, :].rearrange("p t m j -> p (t m j)"))
        quantise_x(0, EARLY_CHUNKS, NCH)
        quantise_x(1, 0, NCH // 2)
        quantise_x(1, NCH // 2, NCH)

        def first_product(s, c):
            bank = psum.tile([P, PACK, CH], F32, name="bank")
            for t in range(PACK):
                cols = slice(t * P, (t + 1) * P)
                nc.tensor.matmul_mx(out=bank[:, t, :], lhsT=w1_codes[:, cols].bitcast(FP8X4), lhsT_scale=w1_scales[:, cols],
                                    rhs=x_codes[s][:, c * CH : (c + 1) * CH].bitcast(FP8X4),
                                    rhs_scale=x_scales(s, c, c + 1), start=True, stop=True)
            return bank

        banks = {}
        for step in range(NCH + SIDE_LEAD):
            for s, c in ((1, step - SIDE_LEAD), (0, step)):
                if 0 <= c < NCH:
                    banks[s, c] = first_product(s, c)

        for q in range(P // QUADRANT):
            if q != LATE_RUN:
                load_scale_rows(q, 0, N)

        out_rows = out.rearrange("(half p) v -> p half v", p=P)
        h_first = [ring.tile([P, CH, PACK], F32, name="h_first") for c in range(NCH)]
        diff = [ring.tile([P, CH, PACK], BF16, name="diff", align_bytes=64) for c in range(NCH)]
        z = [ring.tile([P, CH * PACK], BF16, name="z", align_bytes=64) for c in range(NCH)]
        z_codes = [ring.tile([P, CH], U32, name="z_codes", align_bytes=64) for c in range(NCH)]
        z_scales = [ring.tile([P, CH], U8, name="z_scales", align_bytes=64) for c in range(NCH)]

        def relu(c):
            sums = banks[0, c][:].rearrange("p t v -> p v t")
            if c == VECTOR_RELU:
                nc.vector.tensor_scalar(h_first[c][:], sums, 0.0, None, ALU.max)
            else:
                nc.scalar.activation(h_first[c][:], sums, ACT.Relu)

        def difference(c):
            nc.vector.scalar_tensor_tensor(diff[c][:], banks[1, c][:].rearrange("p t v -> p v t"), 0.0, h_first[c][:],
                                           ALU.max, ALU.subtract)

        def flat_diff(c):
            return diff[c][:].rearrange("p v t -> p (v t)")

        def magnitude_on_scalar(c, width):
            nc.scalar.activation(z[c][:, 0:width], flat_diff(c)[:, 0:width], ACT.Abs)

        def quantise_z(c):
            nc.vector.quantize_mx(out=z_codes[c][:].bitcast(FP8X4), scales=z_scales[c][:], in_=z[c][:])

        def second_product(acc, c, half):
            nc.tensor.matmul_mx(out=acc, lhsT=w2_codes[:, 2 * P * half : 2 * P * (half + 1)].bitcast(FP4X4),
                                lhsT_scale=w2_scale_rows[:, P * half : P * (half + 1)],
                                rhs=z_codes[c][:].bitcast(FP8X4), rhs_scale=z_scales[c][:], start=True, stop=True)

        def finish(c, copy):
            acc = psum.tile([P, PACK, CH], F32, name="bank")
            for half in range(N // P):
                second_product(acc[:, half, :], c, half)
            res = ring.tile([P, N // P, CH], F32, name="res", align_bytes=DMA_ALIGN)
            copy(res[:], acc[:, 0 : N // P, :])
            nc.sync.dma_start(out_rows[:, :, c * CH : (c + 1) * CH], res[:])

        def finish_in_halves(c):
            for half, copy in enumerate((nc.scalar.copy, nc.vector.tensor_copy)):
                acc = psum.tile([P, PACK, CH], F32, name="bank")
                second_product(acc[:, 0, :], c, half)
                part = ring.tile([P, CH], F32, name="part", align_bytes=DMA_ALIGN)
                copy(part[:], acc[:, 0, :])
                nc.sync.dma_start(out_rows[:, half, c * CH : (c + 1) * CH], part[:])

        last = NCH - 1
        for c in range(NCH):
            relu(c)
        for c in range(last):
            difference(c)
        for c in range(last):
            magnitude_on_scalar(c, CH * PACK)
        quantise_z(0)
        difference(last)
        finish(0, nc.scalar.copy)
        quantise_z(1)
        magnitude_on_scalar(last, MAG_SCALAR)
        rest = flat_diff(last)[:, MAG_SCALAR:]
        nc.vector.scalar_tensor_tensor(z[last][:, MAG_SCALAR:], rest, -1.0, rest, ALU.mult, ALU.max)
        finish(1, nc.scalar.copy)
        for c in range(2, NCH):
            quantise_z(c)
        finish_in_halves(last - 1)
        finish_in_halves(last)
